import numpy as np
import ml_dtypes


def mxq(x, axis, fmt="e4m3"):
    dtype, down = {"e4m3": (ml_dtypes.float8_e4m3fn, 7), "e5m2": (ml_dtypes.float8_e5m2, 14)}[fmt]
    v = np.moveaxis(np.asarray(x, np.float32).astype(ml_dtypes.bfloat16).astype(np.float64), axis, -1)
    blocks = v.reshape(v.shape[:-1] + (-1, 32))
    amax = np.abs(blocks).max(-1, keepdims=True)
    byte = np.maximum(np.where(amax > 0, np.frexp(amax)[1] - 1 + 127, 0) - down, 1)
    scale = np.exp2(byte - 127.0)
    codes = (blocks / scale).astype(np.float32).astype(dtype).astype(np.float64)
    return np.moveaxis((codes * scale).reshape(v.shape), -1, axis)


WIDE = False


def mx_kscale(k):
    if not WIDE:
        return np.ones(k)
    levels = np.array([10, -10, 5, -5, 0])
    if k % 512:
        return np.exp2(np.random.permutation(np.resize(levels, k // 32))).repeat(32)
    a = np.empty((k // 512, 16))
    for p in range(k // 512):
        a[p, :8] = np.random.permutation(np.resize(levels, 8))
        for g in range(8):
            far = levels[np.abs(levels - a[p, g]) >= 10]
            a[p, g + 8] = far[np.random.randint(len(far))]
    return np.exp2(a.ravel()).repeat(32)


def f64(x):
    return np.asarray(x).astype(np.float64)


def striped(idx):
    return np.tile(idx.reshape(-1, 16).T, (8, 1)).astype(np.uint16)


def unstriped(offs):
    return offs[:16].T.reshape(-1).astype(np.int64)


E2M1 = np.array([0.0, 0.5, 1.0, 1.5, 2.0, 3.0, 4.0, 6.0, -0.0, -0.5, -1.0, -1.5, -2.0, -3.0, -4.0, -6.0])


def pack_weight(w, fmt):
    k, n = w.shape
    w = f64(np.asarray(w, np.float32).astype(ml_dtypes.bfloat16)).reshape(k // 32, 32, n)
    amax = np.abs(w).max(1)
    if fmt == "e4m3":
        byte = np.frexp(amax)[1] - 1 + 127 - 7
    else:
        mant, ex = np.frexp(amax / 6.0)
        byte = np.where(mant > 0.5, ex, ex - 1) + 127
    byte = np.clip(np.where(amax > 0, byte, 1), 1, 254)
    scaled = (w * np.exp2(127.0 - byte)[:, None, :]).reshape(k, n).astype(np.float32)
    by_word = np.ascontiguousarray(scaled.reshape(k // 512, 128, 4, n).transpose(0, 1, 3, 2))
    if fmt == "e4m3":
        words = by_word.astype(ml_dtypes.float8_e4m3fn).view(np.uint8)
    else:
        c = by_word.astype(ml_dtypes.float4_e2m1fn).view(np.uint8) & 0xF
        words = (c[..., 0::2] | (c[..., 1::2] << 4)).reshape(k // 512, 128, 2 * n)
    return np.ascontiguousarray(words), np.ascontiguousarray(byte.astype(np.uint8).reshape(k // 512, 16, n))


def unpack_weight(words, scales, fmt):
    g, _, n = scales.shape
    words = np.ascontiguousarray(words).reshape(g, 128, n, -1)
    if fmt == "e4m3":
        vals = words.view(ml_dtypes.float8_e4m3fn).astype(np.float64)
    else:
        nib = np.empty((g, 128, n, 4), np.uint8)
        nib[..., 0::2] = words & 0xF
        nib[..., 1::2] = words >> 4
        vals = E2M1[nib]
    vals = vals * np.repeat(np.exp2(scales.astype(np.float64) - 127.0), 8, axis=1)[..., None]
    return vals.transpose(0, 1, 3, 2).reshape(g * 512, n)


def relu(v):
    return np.maximum(v, 0.0)


K, T, E, C, H, N = 512, 640, 10, 128, 512, 128


def by_expert(wq, xq):
    return np.concatenate([wq[e].T @ xq[:, e * C:(e + 1) * C] for e in range(E)], axis=1)


def setup_inputs():
    n = np.random.standard_normal
    s = mx_kscale(K)[:, None]
    u = mx_kscale(H)
    first = np.random.permutation(np.repeat(np.arange(E), T // E))
    second = (first + 1 + np.random.permutation(np.repeat(np.arange(E - 1), -(-T // (E - 1)))[:T])) % E
    while np.bincount(second, minlength=E).max() != T // E:
        load = np.bincount(second, minlength=E); hi, lo = int(load.argmax()), int(load.argmin())
        t = np.flatnonzero((second == hi) & (first != lo))[0]; second[t] = lo
    slot_token = np.empty(E * C, np.int64); pos = np.empty((2, T), np.int64); fill = np.zeros(E, np.int64)
    place = np.stack([np.random.permutation(C) for _ in range(E)])
    for r, deal in enumerate((first, second)):
        for t in np.random.permutation(T):
            e = deal[t]; j = e * C + place[e, fill[e]]; fill[e] += 1; slot_token[j] = t; pos[r, t] = j
    g = np.random.uniform(0.2, 0.8, T)
    w1 = [pack_weight(m, "e2m1") for m in n((E + 1, K, H)) / np.sqrt(K) / s[None] * u[None, None, :]]
    w2 = [pack_weight(m, "e2m1") for m in n((E + 1, H, N)) / np.sqrt(H) / u[None, :, None]]
    x = pack_weight(n((K, T)) * s, "e4m3")
    return {
        "x_words": x[0],
        "x_scales": x[1],
        "w1_words": np.stack([m[0] for m in w1]),
        "w1_scales": np.stack([m[1] for m in w1]),
        "w2_words": np.stack([m[0] for m in w2]),
        "w2_scales": np.stack([m[1] for m in w2]),
        "gate": np.stack([np.tile(g, (N, 1)), np.tile(1.0 - g, (N, 1))]).astype(np.float32),
        "offs": striped(slot_token),
        "pos1": striped(pos[0]),
        "pos2": striped(pos[1]),
    }


def reference(x_words, x_scales, w1_words, w1_scales, w2_words, w2_scales, gate, offs, pos1, pos2):
    idx = unstriped(offs)
    w1 = np.stack([unpack_weight(w1_words[e], w1_scales[e], "e2m1") for e in range(E + 1)])
    w2 = np.stack([unpack_weight(w2_words[e], w2_scales[e], "e2m1") for e in range(E + 1)])
    w1q, w2q = w1, w2
    xs = unpack_weight(x_words, x_scales, "e4m3")
    hs = relu(w1q[E].T @ xs)
    ys = w2q[E].T @ mxq(hs, 0, "e4m3")
    xq = unpack_weight(x_words, x_scales, "e4m3")[:, idx]
    h = relu(by_expert(w1q, xq))
    y = by_expert(w2q, mxq(h, 0, "e4m3"))
    return ys + f64(gate[0]) * y[:, unstriped(pos1)] + f64(gate[1]) * y[:, unstriped(pos2)]

@@ -1,0 +1,199 @@
+from contextlib import ExitStack
+
+import concourse.mybir as mybir
+from concourse.masks import make_identity
+
+K, T, E, C, H, N = 512, 640, 10, 128, 512, 128
+SLOTS = E * C
+FLOPS = 2 * (SLOTS + T) * (K * H + H * N)
+
+F32 = mybir.dt.float32
+BF16 = mybir.dt.bfloat16
+I32 = mybir.dt.int32
+U32 = mybir.dt.uint32
+U16 = mybir.dt.uint16
+U8 = mybir.dt.uint8
+FP8X4 = mybir.dt.float8_e4m3fn_x4
+FP4X4 = mybir.dt.float4_e2m1fn_x4
+RELU = mybir.ActivationFunctionType.Relu
+MULT = mybir.AluOpType.mult
+ADD = mybir.AluOpType.add
+
+P = 128
+LIST_ROWS = 16
+W1_LOADS = ((0, 2), (2, 6), (6, 11))
+GROUPS = ((0, 1), (2, 3), (4, 5), (6, 7), (8,), (9,))
+
+
+def load_scale_rows(nc, plane, rows):
+    for quad in range(4):
+        nc.sync.dma_start(
+            out=plane[32 * quad : 32 * quad + 4].bitcast(I32), in_=rows[4 * quad : 4 * quad + 4].bitcast(I32)
+        )
+
+
+def tile_moe_shr_mlp_relu_kernel(
+    tc, x_words, x_scales, w1_words, w1_scales, w2_words, w2_scales, gate, offs, pos1, pos2, out
+):
+    nc = tc.nc
+    with ExitStack() as ctx:
+        lists = ctx.enter_context(tc.tile_pool(name="lists", bufs=1))
+        keep = ctx.enter_context(tc.tile_pool(name="keep", bufs=1))
+        ring = ctx.enter_context(tc.tile_pool(name="ring", bufs=3))
+        psum_a = ctx.enter_context(tc.psum_pool(name="psum_a", bufs=3))
+        psum_t = ctx.enter_context(tc.psum_pool(name="psum_t", bufs=2))
+        psum_y = ctx.enter_context(tc.psum_pool(name="psum_y", bufs=3))
+
+        offs_sb = lists.tile([P, SLOTS // LIST_ROWS], U16, name="offs_sb")
+        pos1_sb = lists.tile([P, T // LIST_ROWS], U16, name="pos1_sb")
+        pos2_sb = lists.tile([P, T // LIST_ROWS], U16, name="pos2_sb")
+
+        x_codes = keep.tile([P, T], I32, name="x_codes", align_bytes=64)
+        x_plane = keep.tile([P, T], U8, name="x_plane", align_bytes=64)
+        w1_plane = keep.tile([P, E + 1, H], U8, name="w1_plane", align_bytes=64)
+        w2_plane = keep.tile([P, E + 1, N], U8, name="w2_plane", align_bytes=64)
+        ones_diag = keep.tile([P, P], F32, name="ones_diag", tag="reuse1", align_bytes=64)
+        identity = keep.tile([P, P], F32, name="identity")
+        y_slots = keep.tile([P, SLOTS], F32, name="y_slots")
+
+        nc.gpsimd.memset(x_plane[:].bitcast(I32), 0)
+        nc.vector.memset(w1_plane[:].bitcast(I32), 0)
+        make_identity(nc, ones_diag[:])
+        nc.gpsimd.memset(w2_plane[:].bitcast(I32), 0)
+        nc.scalar.activation(out=identity[:], in_=ones_diag[:], func=RELU)
+
+        first_w1 = keep.tile([P, 2, 2 * H], U8, name="first_w1", tag="reuse0", align_bytes=64)
+        later = keep.tile([P, (E - 1) * 2 * H], U8, name="later", tag="reuse1", align_bytes=64)
+        w1_codes = [first_w1[:]] + [
+            later[:, (a - 2) * 2 * H : (b - 2) * 2 * H].rearrange("p (e b) -> p e b", b=2 * H) for a, b in W1_LOADS[1:]
+        ]
+
+        def load_w1_codes(n):
+            a, b = W1_LOADS[n]
+            nc.sync.dma_start(
+                out=w1_codes[n].bitcast(I32), in_=w1_words[a:b, 0].rearrange("e p b -> p e b").bitcast(I32)
+            )
+
+        nc.sync.dma_start(offs_sb[:], offs)
+        nc.sync.dma_start(out=x_codes[:], in_=x_words[0].rearrange("p t r -> p (t r)").bitcast(I32))
+        load_scale_rows(nc, x_plane, x_scales[0])
+        load_w1_codes(0)
+        load_scale_rows(nc, w1_plane, w1_scales[:, 0].rearrange("e q i -> q e i"))
+        nc.sync.dma_start(pos1_sb[:], pos1)
+        nc.sync.dma_start(pos2_sb[:], pos2)
+        load_w1_codes(1)
+        load_w1_codes(2)
+        load_scale_rows(nc, w2_plane, w2_scales[:, 0].rearrange("e q n -> q e n"))
+
+        def w1_of(e):
+            n = [i for i, (a, b) in enumerate(W1_LOADS) if a <= e < b][0]
+            return (
+                w1_codes[n][:, e - W1_LOADS[n][0], :].bitcast(FP4X4),
+                w1_plane[:, e, :],
+            )
+
+        slot_tokens = []
+
+        def gather(width):
+            start = C * len(slot_tokens)
+            entries = offs_sb[:, start // LIST_ROWS : (start + width) // LIST_ROWS]
+            if start == 0:
+                codes = keep.tile([P, width], U32, name="first_codes", align_bytes=64)
+                plane = keep.tile([P, width], U8, name="first_plane", tag="reuse3", align_bytes=64)
+            else:
+                codes = ring.tile([P, width], U32, name="slot_codes", align_bytes=64)
+                plane = ring.tile([P, width], U8, name="slot_plane", align_bytes=64)
+            nc.vector.tensor_copy(out=codes[:], in_=x_codes[:].bitcast(U32).indirect(entries))
+            nc.vector.tensor_copy(out=plane[:], in_=x_plane[:].indirect(entries))
+            for c in range(0, width, C):
+                slot_tokens.append((codes[:, c : c + C].bitcast(FP8X4), plane[:, c : c + C]))
+
+        def first_layer(codes, plane, e):
+            w_codes, w_plane = w1_of(e)
+            a_sums = psum_a.tile([C, H], F32, name="a_sums")
+            nc.tensor.matmul_mx(
+                out=a_sums[:], lhsT=codes, lhsT_scale=plane, rhs=w_codes, rhs_scale=w_plane, start=True, stop=True
+            )
+            return a_sums
+
+        def hidden(tag, sums, copy_out):
+            count = len(sums)
+            turned = psum_t.tile([P, 2, 2, C], F32, name="turned")
+            for j, a_sums in enumerate(sums):
+                h_rows = keep.tile([C, H], BF16, name="h_rows%s_%d" % (tag, j))
+                nc.scalar.activation(
+                    out=h_rows[:].rearrange("s (u q d) -> s u q d", u=2, d=2),
+                    in_=a_sums[:].rearrange("s (q u d) -> s u q d", u=2, d=2),
+                    func=RELU,
+                )
+                pairs = h_rows[:].bitcast(F32)
+                for u in range(2):
+                    nc.tensor.transpose(turned[:, j, u, :], pairs[:, u * P : (u + 1) * P], identity[:])
+            grouped = keep.tile([P, count * C * 4], BF16, name="grouped%s" % tag, align_bytes=64)
+            copy_out(
+                out=grouped[:].bitcast(F32).rearrange("q (j s u) -> q j s u", j=count, u=2),
+                in_=turned[:, 0:count].rearrange("q j u s -> q j s u"),
+            )
+            h_codes = keep.tile([P, count * C], U32, name="h_codes%s" % tag, align_bytes=64)
+            h_plane = keep.tile([P, count * C], U8, name="h_plane%s" % tag, align_bytes=64)
+            nc.vector.quantize_mx(out=h_codes[:].bitcast(FP8X4), scales=h_plane[:], in_=grouped[:])
+            return h_codes, h_plane
+
+        def second_layer(sums, e, h_codes, h_plane):
+            nc.tensor.matmul_mx(
+                out=sums,
+                lhsT=w2_codes[:, e, :].bitcast(FP4X4),
+                lhsT_scale=w2_plane[:, e, :],
+                rhs=h_codes.bitcast(FP8X4),
+                rhs_scale=h_plane,
+                start=True,
+                stop=True,
+            )
+
+        for width in (C, C, 2 * C, 2 * C):
+            gather(width)
+        first_sums = [first_layer(*slot_tokens[e], e) for e in (0, 1)]
+        w2_codes = keep.tile([P, E + 1, 2 * N], U8, name="w2_codes", tag="reuse3", align_bytes=64)
+        nc.sync.dma_start(out=w2_codes[:].bitcast(I32), in_=w2_words[:, 0].rearrange("e p b -> p e b").bitcast(I32))
+        gate_sb = keep.tile([P, 2, T], F32, name="gate_sb", tag="reuse0", align_bytes=64)
+        nc.sync.dma_start(out=gate_sb[:], in_=gate.rearrange("g p t -> p g t"))
+
+        for experts in GROUPS:
+            first = experts[0]
+            sums = first_sums if first == 0 else [first_layer(*slot_tokens[e], e) for e in experts]
+            if len(slot_tokens) < E:
+                gather(2 * C)
+            copy_out = nc.scalar.copy if first == 0 else nc.vector.tensor_copy
+            h_codes, h_plane = hidden("r%d" % first, sums, copy_out)
+            y_sums = psum_y.tile([N, 2 * C], F32, name="y_sums")
+            for j, e in enumerate(experts):
+                cols = slice(j * C, (j + 1) * C)
+                second_layer(y_sums[:, cols], e, h_codes[:, cols], h_plane[:, cols])
+            width = C * len(experts)
+            nc.scalar.copy(out=y_slots[:, C * first : C * first + width], in_=y_sums[:, 0:width])
+
+        for t0 in range(0, T, 2 * C):
+            width = min(2 * C, T - t0)
+            tokens = slice(t0, t0 + width)
+            sums = [
+                first_layer(x_codes[:, c : c + C].bitcast(FP8X4), x_plane[:, c : c + C], E)
+                for c in range(t0, t0 + width, C)
+            ]
+            h_codes, h_plane = hidden("s%d" % t0, sums, nc.scalar.copy)
+            y_sums = psum_y.tile([N, 2 * C], F32, name="y_sums")
+            second_layer(y_sums[:, 0:width], E, h_codes[:], h_plane[:])
+
+            entries = slice(t0 // LIST_ROWS, (t0 + width) // LIST_ROWS)
+            first = keep.tile([N, width], F32, name="first%d" % t0)
+            second = keep.tile([N, width], F32, name="second%d" % t0)
+            routed = keep.tile([N, width], F32, name="routed%d" % t0)
+            result = keep.tile([N, width], F32, name="result%d" % t0)
+            nc.vector.tensor_tensor(
+                out=first[:], in0=y_slots[:].indirect(pos1_sb[:, entries]), in1=gate_sb[:, 0, tokens], op=MULT
+            )
+            nc.vector.tensor_tensor(
+                out=second[:], in0=y_slots[:].indirect(pos2_sb[:, entries]), in1=gate_sb[:, 1, tokens], op=MULT
+            )
+            nc.vector.tensor_tensor(out=routed[:], in0=first[:], in1=second[:], op=ADD)
+            nc.vector.tensor_tensor(out=result[:], in0=routed[:], in1=y_sums[:, 0:width], op=ADD)
+            nc.sync.dma_start(out=out[:, tokens], in_=result[:])

@@ -21,7 +21,7 @@ ADD = mybir.AluOpType.add
 
 P = 128
 LIST_ROWS = 16
-W1_LOADS = ((0, 2), (2, 6), (6, 11))
+W1_LOADS = ((0, 4), (4, 11))
 GROUPS = ((0, 1), (2, 3), (4, 5), (6, 7), (8,), (9,))
 
 
@@ -39,10 +39,8 @@ def tile_moe_shr_mlp_relu_kernel(
     with ExitStack() as ctx:
         lists = ctx.enter_context(tc.tile_pool(name="lists", bufs=1))
         keep = ctx.enter_context(tc.tile_pool(name="keep", bufs=1))
-        ring = ctx.enter_context(tc.tile_pool(name="ring", bufs=3))
-        psum_a = ctx.enter_context(tc.psum_pool(name="psum_a", bufs=3))
-        psum_t = ctx.enter_context(tc.psum_pool(name="psum_t", bufs=2))
-        psum_y = ctx.enter_context(tc.psum_pool(name="psum_y", bufs=3))
+        ring = ctx.enter_context(tc.tile_pool(name="ring", bufs=2))
+        psum = ctx.enter_context(tc.psum_pool(name="psum", bufs=1))
 
         offs_sb = lists.tile([P, SLOTS // LIST_ROWS], U16, name="offs_sb")
         pos1_sb = lists.tile([P, T // LIST_ROWS], U16, name="pos1_sb")
@@ -50,46 +48,51 @@ def tile_moe_shr_mlp_relu_kernel(
 
         x_codes = keep.tile([P, T], I32, name="x_codes", align_bytes=64)
         x_plane = keep.tile([P, T], U8, name="x_plane", align_bytes=64)
-        w1_plane = keep.tile([P, E + 1, H], U8, name="w1_plane", align_bytes=64)
+        w1_codes = [keep.tile([P, b - a, 2 * H], U8, name="w1_codes%d" % a, align_bytes=64) for a, b in W1_LOADS]
+        w1_planes = [keep.tile([P, b - a, H], U8, name="w1_plane%d" % a, align_bytes=64) for a, b in W1_LOADS]
+        w2_codes = keep.tile([P, E + 1, 2 * N], U8, name="w2_codes", align_bytes=64)
         w2_plane = keep.tile([P, E + 1, N], U8, name="w2_plane", align_bytes=64)
-        ones_diag = keep.tile([P, P], F32, name="ones_diag", tag="reuse1", align_bytes=64)
+        gate_sb = keep.tile([P, 2, T], F32, name="gate_sb")
+        ones_diag = keep.tile([P, P], F32, name="ones_diag")
         identity = keep.tile([P, P], F32, name="identity")
         y_slots = keep.tile([P, SLOTS], F32, name="y_slots")
 
         nc.gpsimd.memset(x_plane[:].bitcast(I32), 0)
-        nc.vector.memset(w1_plane[:].bitcast(I32), 0)
+        nc.vector.memset(w1_planes[0][:].bitcast(I32), 0)
+        nc.gpsimd.memset(w1_planes[1][:].bitcast(I32), 0)
+        nc.vector.memset(w2_plane[:].bitcast(I32), 0)
         make_identity(nc, ones_diag[:])
-        nc.gpsimd.memset(w2_plane[:].bitcast(I32), 0)
         nc.scalar.activation(out=identity[:], in_=ones_diag[:], func=RELU)
-
-        first_w1 = keep.tile([P, 2, 2 * H], U8, name="first_w1", tag="reuse0", align_bytes=64)
-        later = keep.tile([P, (E - 1) * 2 * H], U8, name="later", tag="reuse1", align_bytes=64)
-        w1_codes = [first_w1[:]] + [
-            later[:, (a - 2) * 2 * H : (b - 2) * 2 * H].rearrange("p (e b) -> p e b", b=2 * H) for a, b in W1_LOADS[1:]
-        ]
 
         def load_w1_codes(n):
             a, b = W1_LOADS[n]
             nc.sync.dma_start(
-                out=w1_codes[n].bitcast(I32), in_=w1_words[a:b, 0].rearrange("e p b -> p e b").bitcast(I32)
+                out=w1_codes[n][:].bitcast(I32), in_=w1_words[a:b, 0].rearrange("e p b -> p e b").bitcast(I32)
             )
 
+        def load_w1_plane(n):
+            a, b = W1_LOADS[n]
+            load_scale_rows(nc, w1_planes[n], w1_scales[a:b, 0].rearrange("e q i -> q e i"))
+
         nc.sync.dma_start(offs_sb[:], offs)
-        nc.sync.dma_start(out=x_codes[:], in_=x_words[0].rearrange("p t r -> p (t r)").bitcast(I32))
         load_scale_rows(nc, x_plane, x_scales[0])
+        nc.sync.dma_start(out=x_codes[:], in_=x_words[0].rearrange("p t r -> p (t r)").bitcast(I32))
         load_w1_codes(0)
-        load_scale_rows(nc, w1_plane, w1_scales[:, 0].rearrange("e q i -> q e i"))
+        load_w1_plane(0)
+        load_w1_codes(1)
+        load_w1_plane(1)
+        nc.sync.dma_start(out=w2_codes[:].bitcast(I32), in_=w2_words[:, 0].rearrange("e p b -> p e b").bitcast(I32))
+        load_scale_rows(nc, w2_plane, w2_scales[:, 0].rearrange("e q n -> q e n"))
         nc.sync.dma_start(pos1_sb[:], pos1)
         nc.sync.dma_start(pos2_sb[:], pos2)
-        load_w1_codes(1)
-        load_w1_codes(2)
-        load_scale_rows(nc, w2_plane, w2_scales[:, 0].rearrange("e q n -> q e n"))
+        nc.sync.dma_start(out=gate_sb[:], in_=gate.rearrange("g p t -> p g t"))
 
         def w1_of(e):
             n = [i for i, (a, b) in enumerate(W1_LOADS) if a <= e < b][0]
+            m = [i for i, (a, b) in enumerate(W1_LOADS) if a <= e < b][0]
             return (
                 w1_codes[n][:, e - W1_LOADS[n][0], :].bitcast(FP4X4),
-                w1_plane[:, e, :],
+                w1_planes[m][:, e - W1_LOADS[m][0], :],
             )
 
         slot_tokens = []
@@ -99,7 +102,7 @@ def tile_moe_shr_mlp_relu_kernel(
             entries = offs_sb[:, start // LIST_ROWS : (start + width) // LIST_ROWS]
             if start == 0:
                 codes = keep.tile([P, width], U32, name="first_codes", align_bytes=64)
-                plane = keep.tile([P, width], U8, name="first_plane", tag="reuse3", align_bytes=64)
+                plane = keep.tile([P, width], U8, name="first_plane", align_bytes=64)
             else:
                 codes = ring.tile([P, width], U32, name="slot_codes", align_bytes=64)
                 plane = ring.tile([P, width], U8, name="slot_plane", align_bytes=64)
@@ -108,24 +111,18 @@ def tile_moe_shr_mlp_relu_kernel(
             for c in range(0, width, C):
                 slot_tokens.append((codes[:, c : c + C].bitcast(FP8X4), plane[:, c : c + C]))
 
-        def first_layer(codes, plane, e):
+        def first_layer(codes, plane, e, bank):
             w_codes, w_plane = w1_of(e)
-            a_sums = psum_a.tile([C, H], F32, name="a_sums")
+            a_sums = psum.tile([C, H], F32, name="a_sums", tag=bank)
             nc.tensor.matmul_mx(
                 out=a_sums[:], lhsT=codes, lhsT_scale=plane, rhs=w_codes, rhs_scale=w_plane, start=True, stop=True
             )
             return a_sums
 
-        def hidden(tag, sums, copy_out):
+        def hidden(tag, sums, copy_out, bank):
             count = len(sums)
-            turned = psum_t.tile([P, 2, 2, C], F32, name="turned")
-            for j, a_sums in enumerate(sums):
-                h_rows = keep.tile([C, H], BF16, name="h_rows%s_%d" % (tag, j))
-                nc.scalar.activation(
-                    out=h_rows[:].rearrange("s (u q d) -> s u q d", u=2, d=2),
-                    in_=a_sums[:].rearrange("s (q u d) -> s u q d", u=2, d=2),
-                    func=RELU,
-                )
+            turned = psum.tile([P, 2, 2, C], F32, name="turned", tag=bank)
+            for j, h_rows in enumerate(sums):
                 pairs = h_rows[:].bitcast(F32)
                 for u in range(2):
                     nc.tensor.transpose(turned[:, j, u, :], pairs[:, u * P : (u + 1) * P], identity[:])
@@ -150,50 +147,96 @@ def tile_moe_shr_mlp_relu_kernel(
                 stop=True,
             )
 
-        for width in (C, C, 2 * C, 2 * C):
-            gather(width)
-        first_sums = [first_layer(*slot_tokens[e], e) for e in (0, 1)]
-        w2_codes = keep.tile([P, E + 1, 2 * N], U8, name="w2_codes", tag="reuse3", align_bytes=64)
-        nc.sync.dma_start(out=w2_codes[:].bitcast(I32), in_=w2_words[:, 0].rearrange("e p b -> p e b").bitcast(I32))
-        gate_sb = keep.tile([P, 2, T], F32, name="gate_sb", tag="reuse0", align_bytes=64)
-        nc.sync.dma_start(out=gate_sb[:], in_=gate.rearrange("g p t -> p g t"))
+        def relu_rows(tag, a_sums):
+            h_rows = keep.tile([C, H], BF16, name="h_rows%s" % tag)
+            nc.scalar.activation(
+                out=h_rows[:].rearrange("s (u q d) -> s u q d", u=2, d=2),
+                in_=a_sums[:].rearrange("s (q u d) -> s u q d", u=2, d=2),
+                func=RELU,
+            )
+            return h_rows
 
-        for experts in GROUPS:
+        for width in (C, C, 2 * C):
+            gather(width)
+
+        a_banks = ["a0", "a1", "a2", "a0", "y0"] + ["a%d" % ((i + 1) % 3) for i in range(10)]
+        t_banks = ["t0", "y0", "t1", "t0", "t1", "t0", "t1", "t0", "t1"]
+        rows = {}
+
+        def rows_of(e):
+            if e not in rows:
+                rows[e] = relu_rows("r%d" % e, first_layer(*slot_tokens[e], e, a_banks[e]))
+            return rows[e]
+
+        hidden_of = {}
+        for n, experts in enumerate(GROUPS):
             first = experts[0]
-            sums = first_sums if first == 0 else [first_layer(*slot_tokens[e], e) for e in experts]
+            group_rows = [rows_of(e) for e in experts]
             if len(slot_tokens) < E:
                 gather(2 * C)
-            copy_out = nc.scalar.copy if first == 0 else nc.vector.tensor_copy
-            h_codes, h_plane = hidden("r%d" % first, sums, copy_out)
-            y_sums = psum_y.tile([N, 2 * C], F32, name="y_sums")
+            if first == 2:
+                rows_of(4)
+            copy_out = nc.scalar.copy if first <= 4 else nc.vector.tensor_copy
+            h_codes, h_plane = hidden("r%d" % first, group_rows, copy_out, t_banks[n])
             for j, e in enumerate(experts):
-                cols = slice(j * C, (j + 1) * C)
-                second_layer(y_sums[:, cols], e, h_codes[:, cols], h_plane[:, cols])
-            width = C * len(experts)
-            nc.scalar.copy(out=y_slots[:, C * first : C * first + width], in_=y_sums[:, 0:width])
+                hidden_of[e] = (h_codes[:, j * C : (j + 1) * C], h_plane[:, j * C : (j + 1) * C])
+            if experts[-1] in (3, 7, 9):
+                e0 = 4 * (experts[-1] // 4)
+                width = C * (experts[-1] + 1 - e0)
+                y_sums = psum.tile([N, 4 * C], F32, name="y_sums", tag="y%d" % (e0 // 4))
+                for e in range(e0, experts[-1] + 1):
+                    second_layer(y_sums[:, (e - e0) * C : (e - e0 + 1) * C], e, *hidden_of[e])
+                copy_out = nc.scalar.copy if e0 < 8 else nc.vector.tensor_copy
+                copy_out(out=y_slots[:, C * e0 : C * e0 + width], in_=y_sums[:, 0:width])
 
-        for t0 in range(0, T, 2 * C):
+        shared_w1 = keep.tile([P, 4, 2 * P], U8, name="shared_w1", align_bytes=64)
+        shared_plane = keep.tile([P, 4, P], U8, name="shared_plane", align_bytes=64)
+        last = E - W1_LOADS[-1][0]
+        nc.vector.tensor_copy(
+            out=shared_w1[:].bitcast(U16).rearrange("p d (c m) -> p c d m", m=8),
+            in_=w1_codes[-1][:, last, :].bitcast(U16).rearrange("p (c m d) -> p c d m", m=8, d=4),
+        )
+        nc.vector.tensor_copy(
+            out=shared_plane[:].rearrange("p d (c m) -> p c d m", m=16),
+            in_=w1_planes[-1][:, last, :].rearrange("p (c m d) -> p c d m", m=16, d=4),
+        )
+        shared_sums = []
+        for n, t0 in enumerate(range(0, T, 2 * C)):
             width = min(2 * C, T - t0)
-            tokens = slice(t0, t0 + width)
-            sums = [
-                first_layer(x_codes[:, c : c + C].bitcast(FP8X4), x_plane[:, c : c + C], E)
-                for c in range(t0, t0 + width, C)
-            ]
-            h_codes, h_plane = hidden("s%d" % t0, sums, nc.scalar.copy)
-            y_sums = psum_y.tile([N, 2 * C], F32, name="y_sums")
+            grouped = keep.tile([P, width, 4], BF16, name="grouped_s%d" % t0, align_bytes=64)
+            for c in range(t0, t0 + width, C):
+                a_sums = psum.tile([P, 4, C], F32, name="a_sums", tag=a_banks[E + c // C])
+                for d in range(4):
+                    nc.tensor.matmul_mx(
+                        out=a_sums[:, d, :],
+                        lhsT=shared_w1[:, d, :].bitcast(FP4X4),
+                        lhsT_scale=shared_plane[:, d, :],
+                        rhs=x_codes[:, c : c + C].bitcast(FP8X4),
+                        rhs_scale=x_plane[:, c : c + C],
+                        start=True,
+                        stop=True,
+                    )
+                nc.scalar.activation(
+                    out=grouped[:, c - t0 : c - t0 + C, :], in_=a_sums[:].rearrange("q d t -> q t d"), func=RELU
+                )
+            h_codes = keep.tile([P, width], U32, name="h_codes_s%d" % t0, align_bytes=64)
+            h_plane = keep.tile([P, width], U8, name="h_plane_s%d" % t0, align_bytes=64)
+            nc.vector.quantize_mx(
+                out=h_codes[:].bitcast(FP8X4), scales=h_plane[:], in_=grouped[:].rearrange("q t d -> q (t d)")
+            )
+            y_sums = psum.tile([N, 2 * C], F32, name="y_sums", tag=("t1", "y0", "y1")[n])
             second_layer(y_sums[:, 0:width], E, h_codes[:], h_plane[:])
+            shared_sums.append(y_sums[:, 0:width])
 
-            entries = slice(t0 // LIST_ROWS, (t0 + width) // LIST_ROWS)
-            first = keep.tile([N, width], F32, name="first%d" % t0)
-            second = keep.tile([N, width], F32, name="second%d" % t0)
-            routed = keep.tile([N, width], F32, name="routed%d" % t0)
-            result = keep.tile([N, width], F32, name="result%d" % t0)
-            nc.vector.tensor_tensor(
-                out=first[:], in0=y_slots[:].indirect(pos1_sb[:, entries]), in1=gate_sb[:, 0, tokens], op=MULT
-            )
-            nc.vector.tensor_tensor(
-                out=second[:], in0=y_slots[:].indirect(pos2_sb[:, entries]), in1=gate_sb[:, 1, tokens], op=MULT
-            )
-            nc.vector.tensor_tensor(out=routed[:], in0=first[:], in1=second[:], op=ADD)
-            nc.vector.tensor_tensor(out=result[:], in0=routed[:], in1=y_sums[:, 0:width], op=ADD)
-            nc.sync.dma_start(out=out[:, tokens], in_=result[:])
+        first = keep.tile([N, T], F32, name="first")
+        nc.vector.tensor_tensor(out=first[:], in0=y_slots[:].indirect(pos1_sb[:]), in1=gate_sb[:, 0, :], op=MULT)
+        for n, t0 in enumerate(range(0, T, 2 * C)):
+            t1 = min(t0 + 2 * C, T)
+            second = keep.tile([N, t1 - t0], F32, name="second%d" % t0)
+            partial = keep.tile([N, t1 - t0], F32, name="partial%d" % t0)
+            result = keep.tile([N, t1 - t0], F32, name="result%d" % t0)
+            entries = pos2_sb[:, t0 // LIST_ROWS : t1 // LIST_ROWS]
+            nc.vector.tensor_tensor(out=second[:], in0=y_slots[:].indirect(entries), in1=gate_sb[:, 1, t0:t1], op=MULT)
+            nc.vector.tensor_tensor(out=partial[:], in0=first[:, t0:t1], in1=shared_sums[n], op=ADD)
+            nc.vector.tensor_tensor(out=result[:], in0=partial[:], in1=second[:], op=ADD)
+            nc.sync.dma_start(out=out[:, t0:t1], in_=result[:])

@@ -21,7 +21,8 @@ ADD = mybir.AluOpType.add
 
 P = 128
 LIST_ROWS = 16
-W1_LOADS = ((0, 4), (4, 11))
+W1_LOADS = ((0, 1), (1, 4), (4, 11))
+W1_SCALE_LOADS = ((0, 4), (4, 11))
 GROUPS = ((0, 1), (2, 3), (4, 5), (6, 7), (8,), (9,))
 
 
@@ -39,7 +40,8 @@ def tile_moe_shr_mlp_relu_kernel(
     with ExitStack() as ctx:
         lists = ctx.enter_context(tc.tile_pool(name="lists", bufs=1))
         keep = ctx.enter_context(tc.tile_pool(name="keep", bufs=1))
-        ring = ctx.enter_context(tc.tile_pool(name="ring", bufs=2))
+        ring = ctx.enter_context(tc.tile_pool(name="ring", bufs=3))
+        ring2 = ctx.enter_context(tc.tile_pool(name="ring2", bufs=2))
         psum = ctx.enter_context(tc.psum_pool(name="psum", bufs=1))
 
         offs_sb = lists.tile([P, SLOTS // LIST_ROWS], U16, name="offs_sb")
@@ -49,7 +51,7 @@ def tile_moe_shr_mlp_relu_kernel(
         x_codes = keep.tile([P, T], I32, name="x_codes", align_bytes=64)
         x_plane = keep.tile([P, T], U8, name="x_plane", align_bytes=64)
         w1_codes = [keep.tile([P, b - a, 2 * H], U8, name="w1_codes%d" % a, align_bytes=64) for a, b in W1_LOADS]
-        w1_planes = [keep.tile([P, b - a, H], U8, name="w1_plane%d" % a, align_bytes=64) for a, b in W1_LOADS]
+        w1_planes = [keep.tile([P, b - a, H], U8, name="w1_plane%d" % a, align_bytes=64) for a, b in W1_SCALE_LOADS]
         w2_codes = keep.tile([P, E + 1, 2 * N], U8, name="w2_codes", align_bytes=64)
         w2_plane = keep.tile([P, E + 1, N], U8, name="w2_plane", align_bytes=64)
         gate_sb = keep.tile([P, 2, T], F32, name="gate_sb")
@@ -71,15 +73,16 @@ def tile_moe_shr_mlp_relu_kernel(
             )
 
         def load_w1_plane(n):
-            a, b = W1_LOADS[n]
+            a, b = W1_SCALE_LOADS[n]
             load_scale_rows(nc, w1_planes[n], w1_scales[a:b, 0].rearrange("e q i -> q e i"))
 
         nc.sync.dma_start(offs_sb[:], offs)
+        load_w1_codes(0)
         load_scale_rows(nc, x_plane, x_scales[0])
         nc.sync.dma_start(out=x_codes[:], in_=x_words[0].rearrange("p t r -> p (t r)").bitcast(I32))
-        load_w1_codes(0)
-        load_w1_plane(0)
         load_w1_codes(1)
+        load_w1_plane(0)
+        load_w1_codes(2)
         load_w1_plane(1)
         nc.sync.dma_start(out=w2_codes[:].bitcast(I32), in_=w2_words[:, 0].rearrange("e p b -> p e b").bitcast(I32))
         load_scale_rows(nc, w2_plane, w2_scales[:, 0].rearrange("e q n -> q e n"))
@@ -89,10 +92,10 @@ def tile_moe_shr_mlp_relu_kernel(
 
         def w1_of(e):
             n = [i for i, (a, b) in enumerate(W1_LOADS) if a <= e < b][0]
-            m = [i for i, (a, b) in enumerate(W1_LOADS) if a <= e < b][0]
+            m = [i for i, (a, b) in enumerate(W1_SCALE_LOADS) if a <= e < b][0]
             return (
                 w1_codes[n][:, e - W1_LOADS[n][0], :].bitcast(FP4X4),
-                w1_planes[m][:, e - W1_LOADS[m][0], :],
+                w1_planes[m][:, e - W1_SCALE_LOADS[m][0], :],
             )
 
         slot_tokens = []
@@ -105,7 +108,7 @@ def tile_moe_shr_mlp_relu_kernel(
                 plane = keep.tile([P, width], U8, name="first_plane", align_bytes=64)
             else:
                 codes = ring.tile([P, width], U32, name="slot_codes", align_bytes=64)
-                plane = ring.tile([P, width], U8, name="slot_plane", align_bytes=64)
+                plane = ring2.tile([P, width], U8, name="slot_plane", align_bytes=64)
             nc.vector.tensor_copy(out=codes[:], in_=x_codes[:].bitcast(U32).indirect(entries))
             nc.vector.tensor_copy(out=plane[:], in_=x_plane[:].indirect(entries))
             for c in range(0, width, C):
@@ -159,7 +162,7 @@ def tile_moe_shr_mlp_relu_kernel(
         for width in (C, C, 2 * C):
             gather(width)
 
-        a_banks = ["a0", "a1", "a2", "a0", "y0"] + ["a%d" % ((i + 1) % 3) for i in range(10)]
+        a_banks = ["a0", "a1", "a2", "a0", "y0", "a1", "a2", "a0", "a1", "a2", "a0", "y0", "a2", "a0", "y0"]
         t_banks = ["t0", "y0", "t1", "t0", "t1", "t0", "t1", "t0", "t1"]
         rows = {}
 
@@ -169,6 +172,13 @@ def tile_moe_shr_mlp_relu_kernel(
             return rows[e]
 
         hidden_of = {}
+
+        def slot_results(e0, e1, bank, copy_out):
+            y_sums = psum.tile([N, 4 * C], F32, name="y_sums", tag=bank)
+            for e in range(e0, e1):
+                second_layer(y_sums[:, (e - e0) * C : (e - e0 + 1) * C], e, *hidden_of[e])
+            copy_out(out=y_slots[:, C * e0 : C * e1], in_=y_sums[:, 0 : C * (e1 - e0)])
+
         for n, experts in enumerate(GROUPS):
             first = experts[0]
             group_rows = [rows_of(e) for e in experts]
@@ -176,29 +186,25 @@ def tile_moe_shr_mlp_relu_kernel(
                 gather(2 * C)
             if first == 2:
                 rows_of(4)
-            copy_out = nc.scalar.copy if first <= 4 else nc.vector.tensor_copy
+            copy_out = nc.scalar.copy if first <= 2 else nc.vector.tensor_copy
             h_codes, h_plane = hidden("r%d" % first, group_rows, copy_out, t_banks[n])
             for j, e in enumerate(experts):
                 hidden_of[e] = (h_codes[:, j * C : (j + 1) * C], h_plane[:, j * C : (j + 1) * C])
-            if experts[-1] in (3, 7, 9):
-                e0 = 4 * (experts[-1] // 4)
-                width = C * (experts[-1] + 1 - e0)
-                y_sums = psum.tile([N, 4 * C], F32, name="y_sums", tag="y%d" % (e0 // 4))
-                for e in range(e0, experts[-1] + 1):
-                    second_layer(y_sums[:, (e - e0) * C : (e - e0 + 1) * C], e, *hidden_of[e])
-                copy_out = nc.scalar.copy if e0 < 8 else nc.vector.tensor_copy
-                copy_out(out=y_slots[:, C * e0 : C * e0 + width], in_=y_sums[:, 0:width])
+            if experts[-1] == 7:
+                rows_of(8)
+                slot_results(0, 4, "a1", nc.scalar.copy)
+                slot_results(4, 8, "y1", nc.scalar.copy)
+        slot_results(8, 10, "y2", nc.vector.tensor_copy)
 
         shared_w1 = keep.tile([P, 4, 2 * P], U8, name="shared_w1", align_bytes=64)
         shared_plane = keep.tile([P, 4, P], U8, name="shared_plane", align_bytes=64)
-        last = E - W1_LOADS[-1][0]
         nc.vector.tensor_copy(
             out=shared_w1[:].bitcast(U16).rearrange("p d (c m) -> p c d m", m=8),
-            in_=w1_codes[-1][:, last, :].bitcast(U16).rearrange("p (c m d) -> p c d m", m=8, d=4),
+            in_=w1_codes[-1][:, E - W1_LOADS[-1][0], :].bitcast(U16).rearrange("p (c m d) -> p c d m", m=8, d=4),
         )
         nc.vector.tensor_copy(
             out=shared_plane[:].rearrange("p d (c m) -> p c d m", m=16),
-            in_=w1_planes[-1][:, last, :].rearrange("p (c m d) -> p c d m", m=16, d=4),
+            in_=w1_planes[-1][:, E - W1_SCALE_LOADS[-1][0], :].rearrange("p (c m d) -> p c d m", m=16, d=4),
         )
         shared_sums = []
         for n, t0 in enumerate(range(0, T, 2 * C)):
@@ -224,7 +230,7 @@ def tile_moe_shr_mlp_relu_kernel(
             nc.vector.quantize_mx(
                 out=h_codes[:].bitcast(FP8X4), scales=h_plane[:], in_=grouped[:].rearrange("q t d -> q (t d)")
             )
-            y_sums = psum.tile([N, 2 * C], F32, name="y_sums", tag=("t1", "y0", "y1")[n])
+            y_sums = psum.tile([N, 2 * C], F32, name="y_sums", tag=("t1", "y1", "a2")[n])
             second_layer(y_sums[:, 0:width], E, h_codes[:], h_plane[:])
             shared_sums.append(y_sums[:, 0:width])
 

@@ -20,10 +20,17 @@ MULT = mybir.AluOpType.mult
 ADD = mybir.AluOpType.add
 
 P = 128
+PACK = 4
 LIST_ROWS = 16
-W1_LOADS = ((0, 1), (1, 4), (4, 11))
-W1_SCALE_LOADS = ((0, 4), (4, 11))
-GROUPS = ((0, 1), (2, 3), (4, 5), (6, 7), (8,), (9,))
+
+EARLY = 7
+GATHERS = ((7, 8), (8, 10), (0, 2), (2, 4), (4, 7))
+GROUPS = ((7,), (8, 9), (0, 1), (2, 3), (4, 5), (6,))
+SUM_BANKS = {7: "a0", 8: "a1", 9: "a2", 0: "y0", 1: "a0", 2: "a1", 3: "a2", 4: "a0", 5: "a1", 6: "a2"}
+TURN_BANKS = ("t0", "y0", "t1", "t0", "t1", "t0")
+SHARED_SUM_BANKS = ("a0", "y0", "a2", "a0", "y0")
+SHARED_RESULT_BANKS = ("t1", "y1", "a2")
+GROUPS_COPIED_BY_SCALAR = 3
 
 
 def load_scale_rows(nc, plane, rows):
@@ -40,8 +47,8 @@ def tile_moe_shr_mlp_relu_kernel(
     with ExitStack() as ctx:
         lists = ctx.enter_context(tc.tile_pool(name="lists", bufs=1))
         keep = ctx.enter_context(tc.tile_pool(name="keep", bufs=1))
-        ring = ctx.enter_context(tc.tile_pool(name="ring", bufs=3))
-        ring2 = ctx.enter_context(tc.tile_pool(name="ring2", bufs=2))
+        plane_ring = ctx.enter_context(tc.tile_pool(name="plane_ring", bufs=3))
+        code_ring = ctx.enter_context(tc.tile_pool(name="code_ring", bufs=2))
         psum = ctx.enter_context(tc.psum_pool(name="psum", bufs=1))
 
         offs_sb = lists.tile([P, SLOTS // LIST_ROWS], U16, name="offs_sb")
@@ -50,8 +57,10 @@ def tile_moe_shr_mlp_relu_kernel(
 
         x_codes = keep.tile([P, T], I32, name="x_codes", align_bytes=64)
         x_plane = keep.tile([P, T], U8, name="x_plane", align_bytes=64)
-        w1_codes = [keep.tile([P, b - a, 2 * H], U8, name="w1_codes%d" % a, align_bytes=64) for a, b in W1_LOADS]
-        w1_planes = [keep.tile([P, b - a, H], U8, name="w1_plane%d" % a, align_bytes=64) for a, b in W1_SCALE_LOADS]
+        early_codes = keep.tile([P, E + 1 - EARLY, 2 * H], U8, name="early_codes", align_bytes=64)
+        early_plane = keep.tile([P, E + 1 - EARLY, H], U8, name="early_plane", align_bytes=64)
+        late_codes = keep.tile([P, EARLY, 2 * H], U8, name="late_codes", align_bytes=64)
+        late_plane = keep.tile([P, EARLY, H], U8, name="late_plane", align_bytes=64)
         w2_codes = keep.tile([P, E + 1, 2 * N], U8, name="w2_codes", align_bytes=64)
         w2_plane = keep.tile([P, E + 1, N], U8, name="w2_plane", align_bytes=64)
         gate_sb = keep.tile([P, 2, T], F32, name="gate_sb")
@@ -60,84 +69,96 @@ def tile_moe_shr_mlp_relu_kernel(
         y_slots = keep.tile([P, SLOTS], F32, name="y_slots")
 
         nc.gpsimd.memset(x_plane[:].bitcast(I32), 0)
-        nc.vector.memset(w1_planes[0][:].bitcast(I32), 0)
-        nc.gpsimd.memset(w1_planes[1][:].bitcast(I32), 0)
+        nc.vector.memset(early_plane[:].bitcast(I32), 0)
+        nc.gpsimd.memset(late_plane[:].bitcast(I32), 0)
         nc.vector.memset(w2_plane[:].bitcast(I32), 0)
         make_identity(nc, ones_diag[:])
         nc.scalar.activation(out=identity[:], in_=ones_diag[:], func=RELU)
 
-        def load_w1_codes(n):
-            a, b = W1_LOADS[n]
-            nc.sync.dma_start(
-                out=w1_codes[n][:].bitcast(I32), in_=w1_words[a:b, 0].rearrange("e p b -> p e b").bitcast(I32)
-            )
-
-        def load_w1_plane(n):
-            a, b = W1_SCALE_LOADS[n]
-            load_scale_rows(nc, w1_planes[n], w1_scales[a:b, 0].rearrange("e q i -> q e i"))
+        def load_words(codes, words):
+            nc.sync.dma_start(out=codes[:].bitcast(I32), in_=words.rearrange("e p b -> p e b").bitcast(I32))
 
         nc.sync.dma_start(offs_sb[:], offs)
-        load_w1_codes(0)
-        load_scale_rows(nc, x_plane, x_scales[0])
         nc.sync.dma_start(out=x_codes[:], in_=x_words[0].rearrange("p t r -> p (t r)").bitcast(I32))
-        load_w1_codes(1)
-        load_w1_plane(0)
-        load_w1_codes(2)
-        load_w1_plane(1)
-        nc.sync.dma_start(out=w2_codes[:].bitcast(I32), in_=w2_words[:, 0].rearrange("e p b -> p e b").bitcast(I32))
-        load_scale_rows(nc, w2_plane, w2_scales[:, 0].rearrange("e q n -> q e n"))
+        load_scale_rows(nc, x_plane, x_scales[0])
+        load_words(early_codes, w1_words[EARLY:, 0])
+        load_scale_rows(nc, early_plane, w1_scales[EARLY:, 0].rearrange("e f i -> f e i"))
+        load_words(late_codes, w1_words[:EARLY, 0])
+        load_scale_rows(nc, late_plane, w1_scales[:EARLY, 0].rearrange("e f i -> f e i"))
+        load_words(w2_codes, w2_words[:, 0])
+        load_scale_rows(nc, w2_plane, w2_scales[:, 0].rearrange("e f n -> f e n"))
         nc.sync.dma_start(pos1_sb[:], pos1)
         nc.sync.dma_start(pos2_sb[:], pos2)
         nc.sync.dma_start(out=gate_sb[:], in_=gate.rearrange("g p t -> p g t"))
 
         def w1_of(e):
-            n = [i for i, (a, b) in enumerate(W1_LOADS) if a <= e < b][0]
-            m = [i for i, (a, b) in enumerate(W1_SCALE_LOADS) if a <= e < b][0]
-            return (
-                w1_codes[n][:, e - W1_LOADS[n][0], :].bitcast(FP4X4),
-                w1_planes[m][:, e - W1_SCALE_LOADS[m][0], :],
-            )
+            if e >= EARLY:
+                return early_codes[:, e - EARLY, :], early_plane[:, e - EARLY, :]
+            return late_codes[:, e, :], late_plane[:, e, :]
 
-        slot_tokens = []
+        tokens_of = {}
 
-        def gather(width):
-            start = C * len(slot_tokens)
-            entries = offs_sb[:, start // LIST_ROWS : (start + width) // LIST_ROWS]
-            if start == 0:
+        def gather(e0, e1):
+            width = C * (e1 - e0)
+            entries = offs_sb[:, C * e0 // LIST_ROWS : C * e1 // LIST_ROWS]
+            if (e0, e1) == GATHERS[0]:
                 codes = keep.tile([P, width], U32, name="first_codes", align_bytes=64)
                 plane = keep.tile([P, width], U8, name="first_plane", align_bytes=64)
             else:
-                codes = ring.tile([P, width], U32, name="slot_codes", align_bytes=64)
-                plane = ring2.tile([P, width], U8, name="slot_plane", align_bytes=64)
+                codes = code_ring.tile([P, width], U32, name="slot_codes", align_bytes=64)
+                plane = plane_ring.tile([P, width], U8, name="slot_plane", align_bytes=64)
             nc.vector.tensor_copy(out=codes[:], in_=x_codes[:].bitcast(U32).indirect(entries))
             nc.vector.tensor_copy(out=plane[:], in_=x_plane[:].indirect(entries))
-            for c in range(0, width, C):
-                slot_tokens.append((codes[:, c : c + C].bitcast(FP8X4), plane[:, c : c + C]))
+            for e in range(e0, e1):
+                cols = slice(C * (e - e0), C * (e - e0 + 1))
+                tokens_of[e] = (codes[:, cols], plane[:, cols])
 
-        def first_layer(codes, plane, e, bank):
+        h_rows_of = {}
+
+        def first_layer(e):
+            codes, plane = tokens_of[e]
             w_codes, w_plane = w1_of(e)
-            a_sums = psum.tile([C, H], F32, name="a_sums", tag=bank)
+            a_sums = psum.tile([C, H], F32, name="a_sums", tag=SUM_BANKS[e])
             nc.tensor.matmul_mx(
-                out=a_sums[:], lhsT=codes, lhsT_scale=plane, rhs=w_codes, rhs_scale=w_plane, start=True, stop=True
+                out=a_sums[:],
+                lhsT=codes.bitcast(FP8X4),
+                lhsT_scale=plane,
+                rhs=w_codes.bitcast(FP4X4),
+                rhs_scale=w_plane,
+                start=True,
+                stop=True,
             )
-            return a_sums
+            h_rows = keep.tile([C, H], BF16, name="h_rows%d" % e)
+            nc.scalar.activation(
+                out=h_rows[:].rearrange("s (u q d) -> s u q d", u=2, d=2),
+                in_=a_sums[:].rearrange("s (q u d) -> s u q d", u=2, d=2),
+                func=RELU,
+            )
+            h_rows_of[e] = h_rows
 
-        def hidden(tag, sums, copy_out, bank):
-            count = len(sums)
+        def quantise(name, grouped, width):
+            h_codes = keep.tile([P, width], U32, name="h_codes" + name, align_bytes=64)
+            h_plane = keep.tile([P, width], U8, name="h_plane" + name, align_bytes=64)
+            nc.vector.quantize_mx(out=h_codes[:].bitcast(FP8X4), scales=h_plane[:], in_=grouped)
+            return h_codes, h_plane
+
+        hidden_of = {}
+
+        def turn_and_quantise(experts, bank, copy_out):
+            count = len(experts)
             turned = psum.tile([P, 2, 2, C], F32, name="turned", tag=bank)
-            for j, h_rows in enumerate(sums):
-                pairs = h_rows[:].bitcast(F32)
+            for j, e in enumerate(experts):
+                pairs = h_rows_of[e][:].bitcast(F32)
                 for u in range(2):
                     nc.tensor.transpose(turned[:, j, u, :], pairs[:, u * P : (u + 1) * P], identity[:])
-            grouped = keep.tile([P, count * C * 4], BF16, name="grouped%s" % tag, align_bytes=64)
+            grouped = keep.tile([P, count * C * PACK], BF16, name="grouped%d" % experts[0], align_bytes=64)
             copy_out(
                 out=grouped[:].bitcast(F32).rearrange("q (j s u) -> q j s u", j=count, u=2),
                 in_=turned[:, 0:count].rearrange("q j u s -> q j s u"),
             )
-            h_codes = keep.tile([P, count * C], U32, name="h_codes%s" % tag, align_bytes=64)
-            h_plane = keep.tile([P, count * C], U8, name="h_plane%s" % tag, align_bytes=64)
-            nc.vector.quantize_mx(out=h_codes[:].bitcast(FP8X4), scales=h_plane[:], in_=grouped[:])
-            return h_codes, h_plane
+            h_codes, h_plane = quantise("%d" % experts[0], grouped[:], count * C)
+            for j, e in enumerate(experts):
+                hidden_of[e] = (h_codes[:, j * C : (j + 1) * C], h_plane[:, j * C : (j + 1) * C])
 
         def second_layer(sums, e, h_codes, h_plane):
             nc.tensor.matmul_mx(
@@ -150,72 +171,50 @@ def tile_moe_shr_mlp_relu_kernel(
                 stop=True,
             )
 
-        def relu_rows(tag, a_sums):
-            h_rows = keep.tile([C, H], BF16, name="h_rows%s" % tag)
-            nc.scalar.activation(
-                out=h_rows[:].rearrange("s (u q d) -> s u q d", u=2, d=2),
-                in_=a_sums[:].rearrange("s (q u d) -> s u q d", u=2, d=2),
-                func=RELU,
-            )
-            return h_rows
-
-        for width in (C, C, 2 * C):
-            gather(width)
-
-        a_banks = ["a0", "a1", "a2", "a0", "y0", "a1", "a2", "a0", "a1", "a2", "a0", "y0", "a2", "a0", "y0"]
-        t_banks = ["t0", "y0", "t1", "t0", "t1", "t0", "t1", "t0", "t1"]
-        rows = {}
-
-        def rows_of(e):
-            if e not in rows:
-                rows[e] = relu_rows("r%d" % e, first_layer(*slot_tokens[e], e, a_banks[e]))
-            return rows[e]
-
-        hidden_of = {}
-
         def slot_results(e0, e1, bank, copy_out):
             y_sums = psum.tile([N, 4 * C], F32, name="y_sums", tag=bank)
             for e in range(e0, e1):
                 second_layer(y_sums[:, (e - e0) * C : (e - e0 + 1) * C], e, *hidden_of[e])
             copy_out(out=y_slots[:, C * e0 : C * e1], in_=y_sums[:, 0 : C * (e1 - e0)])
 
+        for e0, e1 in GATHERS[:3]:
+            gather(e0, e1)
         for n, experts in enumerate(GROUPS):
-            first = experts[0]
-            group_rows = [rows_of(e) for e in experts]
-            if len(slot_tokens) < E:
-                gather(2 * C)
-            if first == 2:
-                rows_of(4)
-            copy_out = nc.scalar.copy if first <= 2 else nc.vector.tensor_copy
-            h_codes, h_plane = hidden("r%d" % first, group_rows, copy_out, t_banks[n])
-            for j, e in enumerate(experts):
-                hidden_of[e] = (h_codes[:, j * C : (j + 1) * C], h_plane[:, j * C : (j + 1) * C])
-            if experts[-1] == 7:
-                rows_of(8)
-                slot_results(0, 4, "a1", nc.scalar.copy)
-                slot_results(4, 8, "y1", nc.scalar.copy)
-        slot_results(8, 10, "y2", nc.vector.tensor_copy)
+            for e in experts:
+                if e not in h_rows_of:
+                    first_layer(e)
+            if n in (1, 2):
+                gather(*GATHERS[n + 2])
+            if n == 1:
+                first_layer(GROUPS[2][0])
+            if n == len(GROUPS) - 1:
+                slot_results(EARLY, E, "a1", nc.scalar.copy)
+                slot_results(0, 4, "y1", nc.scalar.copy)
+            copy_out = nc.scalar.copy if n < GROUPS_COPIED_BY_SCALAR else nc.vector.tensor_copy
+            turn_and_quantise(experts, TURN_BANKS[n], copy_out)
+        slot_results(4, EARLY, "y2", nc.vector.tensor_copy)
 
-        shared_w1 = keep.tile([P, 4, 2 * P], U8, name="shared_w1", align_bytes=64)
-        shared_plane = keep.tile([P, 4, P], U8, name="shared_plane", align_bytes=64)
+        shared_codes = keep.tile([P, PACK, 2 * P], U8, name="shared_codes", align_bytes=64)
+        shared_plane = keep.tile([P, PACK, P], U8, name="shared_plane", align_bytes=64)
+        w_codes, w_plane = w1_of(E)
         nc.vector.tensor_copy(
-            out=shared_w1[:].bitcast(U16).rearrange("p d (c m) -> p c d m", m=8),
-            in_=w1_codes[-1][:, E - W1_LOADS[-1][0], :].bitcast(U16).rearrange("p (c m d) -> p c d m", m=8, d=4),
+            out=shared_codes[:].bitcast(U16).rearrange("p d (c m) -> p c d m", m=8),
+            in_=w_codes.bitcast(U16).rearrange("p (c m d) -> p c d m", m=8, d=PACK),
         )
         nc.vector.tensor_copy(
             out=shared_plane[:].rearrange("p d (c m) -> p c d m", m=16),
-            in_=w1_planes[-1][:, E - W1_SCALE_LOADS[-1][0], :].rearrange("p (c m d) -> p c d m", m=16, d=4),
+            in_=w_plane.rearrange("p (c m d) -> p c d m", m=16, d=PACK),
         )
-        shared_sums = []
+        shared_results = []
         for n, t0 in enumerate(range(0, T, 2 * C)):
             width = min(2 * C, T - t0)
-            grouped = keep.tile([P, width, 4], BF16, name="grouped_s%d" % t0, align_bytes=64)
+            grouped = keep.tile([P, width, PACK], BF16, name="grouped_s%d" % t0, align_bytes=64)
             for c in range(t0, t0 + width, C):
-                a_sums = psum.tile([P, 4, C], F32, name="a_sums", tag=a_banks[E + c // C])
-                for d in range(4):
+                a_sums = psum.tile([P, PACK, C], F32, name="a_sums", tag=SHARED_SUM_BANKS[c // C])
+                for d in range(PACK):
                     nc.tensor.matmul_mx(
                         out=a_sums[:, d, :],
-                        lhsT=shared_w1[:, d, :].bitcast(FP4X4),
+                        lhsT=shared_codes[:, d, :].bitcast(FP4X4),
                         lhsT_scale=shared_plane[:, d, :],
                         rhs=x_codes[:, c : c + C].bitcast(FP8X4),
                         rhs_scale=x_plane[:, c : c + C],
@@ -225,14 +224,10 @@ def tile_moe_shr_mlp_relu_kernel(
                 nc.scalar.activation(
                     out=grouped[:, c - t0 : c - t0 + C, :], in_=a_sums[:].rearrange("q d t -> q t d"), func=RELU
                 )
-            h_codes = keep.tile([P, width], U32, name="h_codes_s%d" % t0, align_bytes=64)
-            h_plane = keep.tile([P, width], U8, name="h_plane_s%d" % t0, align_bytes=64)
-            nc.vector.quantize_mx(
-                out=h_codes[:].bitcast(FP8X4), scales=h_plane[:], in_=grouped[:].rearrange("q t d -> q (t d)")
-            )
-            y_sums = psum.tile([N, 2 * C], F32, name="y_sums", tag=("t1", "y1", "a2")[n])
-            second_layer(y_sums[:, 0:width], E, h_codes[:], h_plane[:])
-            shared_sums.append(y_sums[:, 0:width])
+            h_codes, h_plane = quantise("_s%d" % t0, grouped[:].rearrange("q t d -> q (t d)"), width)
+            ys_sums = psum.tile([N, 2 * C], F32, name="ys_sums", tag=SHARED_RESULT_BANKS[n])
+            second_layer(ys_sums[:, 0:width], E, h_codes[:], h_plane[:])
+            shared_results.append(ys_sums[:, 0:width])
 
         first = keep.tile([N, T], F32, name="first")
         nc.vector.tensor_tensor(out=first[:], in0=y_slots[:].indirect(pos1_sb[:]), in1=gate_sb[:, 0, :], op=MULT)
@@ -243,6 +238,6 @@ def tile_moe_shr_mlp_relu_kernel(
             result = keep.tile([N, t1 - t0], F32, name="result%d" % t0)
             entries = pos2_sb[:, t0 // LIST_ROWS : t1 // LIST_ROWS]
             nc.vector.tensor_tensor(out=second[:], in0=y_slots[:].indirect(entries), in1=gate_sb[:, 1, t0:t1], op=MULT)
-            nc.vector.tensor_tensor(out=partial[:], in0=first[:, t0:t1], in1=shared_sums[n], op=ADD)
+            nc.vector.tensor_tensor(out=partial[:], in0=first[:, t0:t1], in1=shared_results[n], op=ADD)
             nc.vector.tensor_tensor(out=result[:], in0=partial[:], in1=second[:], op=ADD)
             nc.sync.dma_start(out=out[:, t0:t1], in_=result[:])

@@ -24,6 +24,7 @@ PACK = 4
 LIST_ROWS = 16
 
 EARLY = 7
+MIDDLE = 2
 GATHERS = ((7, 8), (8, 10), (0, 2), (2, 4), (4, 7))
 GROUPS = ((7,), (8, 9), (0, 1), (2, 3), (4, 5), (6,))
 SUM_BANKS = {7: "a0", 8: "a1", 9: "a2", 0: "y0", 1: "a0", 2: "a1", 3: "a2", 4: "a0", 5: "a1", 6: "a2"}
@@ -34,10 +35,8 @@ GROUPS_COPIED_BY_SCALAR = 3
 
 
 def load_scale_rows(nc, plane, rows):
-    for quad in range(4):
-        nc.sync.dma_start(
-            out=plane[32 * quad : 32 * quad + 4].bitcast(I32), in_=rows[4 * quad : 4 * quad + 4].bitcast(I32)
-        )
+    for r in range(4):
+        nc.sync.dma_start(out=plane[r:P:32].bitcast(I32), in_=rows[r:16:4].bitcast(I32))
 
 
 def tile_moe_shr_mlp_relu_kernel(
@@ -59,7 +58,8 @@ def tile_moe_shr_mlp_relu_kernel(
         x_plane = keep.tile([P, T], U8, name="x_plane", align_bytes=64)
         early_codes = keep.tile([P, E + 1 - EARLY, 2 * H], U8, name="early_codes", align_bytes=64)
         early_plane = keep.tile([P, E + 1 - EARLY, H], U8, name="early_plane", align_bytes=64)
-        late_codes = keep.tile([P, EARLY, 2 * H], U8, name="late_codes", align_bytes=64)
+        middle_codes = keep.tile([P, MIDDLE, 2 * H], U8, name="middle_codes", align_bytes=64)
+        late_codes = keep.tile([P, EARLY - MIDDLE, 2 * H], U8, name="late_codes", align_bytes=64)
         late_plane = keep.tile([P, EARLY, H], U8, name="late_plane", align_bytes=64)
         w2_codes = keep.tile([P, E + 1, 2 * N], U8, name="w2_codes", align_bytes=64)
         w2_plane = keep.tile([P, E + 1, N], U8, name="w2_plane", align_bytes=64)
@@ -83,8 +83,9 @@ def tile_moe_shr_mlp_relu_kernel(
         load_scale_rows(nc, x_plane, x_scales[0])
         load_words(early_codes, w1_words[EARLY:, 0])
         load_scale_rows(nc, early_plane, w1_scales[EARLY:, 0].rearrange("e f i -> f e i"))
-        load_words(late_codes, w1_words[:EARLY, 0])
+        load_words(middle_codes, w1_words[:MIDDLE, 0])
         load_scale_rows(nc, late_plane, w1_scales[:EARLY, 0].rearrange("e f i -> f e i"))
+        load_words(late_codes, w1_words[MIDDLE:EARLY, 0])
         load_words(w2_codes, w2_words[:, 0])
         load_scale_rows(nc, w2_plane, w2_scales[:, 0].rearrange("e f n -> f e n"))
         nc.sync.dma_start(pos1_sb[:], pos1)
@@ -94,7 +95,9 @@ def tile_moe_shr_mlp_relu_kernel(
         def w1_of(e):
             if e >= EARLY:
                 return early_codes[:, e - EARLY, :], early_plane[:, e - EARLY, :]
-            return late_codes[:, e, :], late_plane[:, e, :]
+            if e < MIDDLE:
+                return middle_codes[:, e, :], late_plane[:, e, :]
+            return late_codes[:, e - MIDDLE, :], late_plane[:, e, :]
 
         tokens_of = {}
 

@@ -16,6 +16,7 @@ U8 = mybir.dt.uint8
 FP8X4 = mybir.dt.float8_e4m3fn_x4
 FP4X4 = mybir.dt.float4_e2m1fn_x4
 RELU = mybir.ActivationFunctionType.Relu
+COPY = mybir.ActivationFunctionType.Copy
 MULT = mybir.AluOpType.mult
 ADD = mybir.AluOpType.add
 
@@ -23,20 +24,17 @@ P = 128
 PACK = 4
 LIST_ROWS = 16
 
-EARLY = 7
-MIDDLE = 2
-GATHERS = ((7, 8), (8, 10), (0, 2), (2, 4), (4, 7))
-GROUPS = ((7,), (8, 9), (0, 1), (2, 3), (4, 5), (6,))
-SUM_BANKS = {7: "a0", 8: "a1", 9: "a2", 0: "y0", 1: "a0", 2: "a1", 3: "a2", 4: "a0", 5: "a1", 6: "a2"}
-TURN_BANKS = ("t0", "y0", "t1", "t0", "t1", "t0")
-SHARED_SUM_BANKS = ("a0", "y0", "a2", "a0", "y0")
-SHARED_RESULT_BANKS = ("t1", "y1", "a2")
-GROUPS_COPIED_BY_SCALAR = 3
+EARLY = 3
+MIDDLE = 7
+GATHERS = ((0, 1), (1, 3), (3, 5), (5, 8), (8, 10))
+GROUPS = ((0, 1), (2, 3), (4, 5), (6, 7), (8,), (9,))
+GROUPS_COPIED_BY_VECTOR = (2, 3)
+SUM_BANKS = ("a0", "a1", "a2", "y2", "y1", "y0", "a0", "a1", "y2", "a2")
 
 
-def load_scale_rows(nc, plane, rows):
+def load_scale_rows(queue, plane, rows):
     for r in range(4):
-        nc.sync.dma_start(out=plane[r:P:32].bitcast(I32), in_=rows[r:16:4].bitcast(I32))
+        queue.dma_start(out=plane[r:P:32].bitcast(I32), in_=rows[r:16:4].bitcast(I32))
 
 
 def tile_moe_shr_mlp_relu_kernel(
@@ -46,8 +44,7 @@ def tile_moe_shr_mlp_relu_kernel(
     with ExitStack() as ctx:
         lists = ctx.enter_context(tc.tile_pool(name="lists", bufs=1))
         keep = ctx.enter_context(tc.tile_pool(name="keep", bufs=1))
-        plane_ring = ctx.enter_context(tc.tile_pool(name="plane_ring", bufs=3))
-        code_ring = ctx.enter_context(tc.tile_pool(name="code_ring", bufs=2))
+        ring = ctx.enter_context(tc.tile_pool(name="ring", bufs=2))
         psum = ctx.enter_context(tc.psum_pool(name="psum", bufs=1))
 
         offs_sb = lists.tile([P, SLOTS // LIST_ROWS], U16, name="offs_sb")
@@ -56,60 +53,59 @@ def tile_moe_shr_mlp_relu_kernel(
 
         x_codes = keep.tile([P, T], I32, name="x_codes", align_bytes=64)
         x_plane = keep.tile([P, T], U8, name="x_plane", align_bytes=64)
-        early_codes = keep.tile([P, E + 1 - EARLY, 2 * H], U8, name="early_codes", align_bytes=64)
-        early_plane = keep.tile([P, E + 1 - EARLY, H], U8, name="early_plane", align_bytes=64)
-        middle_codes = keep.tile([P, MIDDLE, 2 * H], U8, name="middle_codes", align_bytes=64)
-        late_codes = keep.tile([P, EARLY - MIDDLE, 2 * H], U8, name="late_codes", align_bytes=64)
-        late_plane = keep.tile([P, EARLY, H], U8, name="late_plane", align_bytes=64)
+        early_codes = keep.tile([P, EARLY, 2 * H], U8, name="early_codes", align_bytes=64)
+        early_plane = keep.tile([P, EARLY, H], U8, name="early_plane", align_bytes=64)
+        middle_codes = keep.tile([P, MIDDLE - EARLY, 2 * H], U8, name="middle_codes", align_bytes=64)
+        late_codes = keep.tile([P, E + 1 - MIDDLE, 2 * H], U8, name="late_codes", align_bytes=64)
+        late_plane = keep.tile([P, E + 1 - EARLY, H], U8, name="late_plane", align_bytes=64)
         w2_codes = keep.tile([P, E + 1, 2 * N], U8, name="w2_codes", align_bytes=64)
         w2_plane = keep.tile([P, E + 1, N], U8, name="w2_plane", align_bytes=64)
-        gate_sb = keep.tile([P, 2, T], F32, name="gate_sb")
+        gate_sb = keep.tile([P, T], F32, name="gate_sb")
+        gate_col = keep.tile([P, T // C], F32, name="gate_col")
         ones_diag = keep.tile([P, P], F32, name="ones_diag")
         identity = keep.tile([P, P], F32, name="identity")
         y_slots = keep.tile([P, SLOTS], F32, name="y_slots")
 
         nc.gpsimd.memset(x_plane[:].bitcast(I32), 0)
         nc.vector.memset(early_plane[:].bitcast(I32), 0)
-        nc.gpsimd.memset(late_plane[:].bitcast(I32), 0)
-        nc.vector.memset(w2_plane[:].bitcast(I32), 0)
+        nc.vector.memset(late_plane[:].bitcast(I32), 0)
         make_identity(nc, ones_diag[:])
+        nc.gpsimd.memset(w2_plane[:].bitcast(I32), 0)
         nc.scalar.activation(out=identity[:], in_=ones_diag[:], func=RELU)
 
         def load_words(codes, words):
             nc.sync.dma_start(out=codes[:].bitcast(I32), in_=words.rearrange("e p b -> p e b").bitcast(I32))
 
         nc.sync.dma_start(offs_sb[:], offs)
+        load_scale_rows(nc.sync, x_plane, x_scales[0])
         nc.sync.dma_start(out=x_codes[:], in_=x_words[0].rearrange("p t r -> p (t r)").bitcast(I32))
-        load_scale_rows(nc, x_plane, x_scales[0])
-        load_words(early_codes, w1_words[EARLY:, 0])
-        load_scale_rows(nc, early_plane, w1_scales[EARLY:, 0].rearrange("e f i -> f e i"))
-        load_words(middle_codes, w1_words[:MIDDLE, 0])
-        load_scale_rows(nc, late_plane, w1_scales[:EARLY, 0].rearrange("e f i -> f e i"))
-        load_words(late_codes, w1_words[MIDDLE:EARLY, 0])
+        load_words(early_codes, w1_words[:EARLY, 0])
+        load_scale_rows(nc.sync, early_plane, w1_scales[:EARLY, 0].rearrange("e f i -> f e i"))
+        load_words(middle_codes, w1_words[EARLY:MIDDLE, 0])
+        load_scale_rows(nc.sync, late_plane, w1_scales[EARLY:, 0].rearrange("e f i -> f e i"))
+        load_words(late_codes, w1_words[MIDDLE:, 0])
         load_words(w2_codes, w2_words[:, 0])
-        load_scale_rows(nc, w2_plane, w2_scales[:, 0].rearrange("e f n -> f e n"))
+        load_scale_rows(nc.gpsimd, w2_plane, w2_scales[:, 0].rearrange("e f n -> f e n"))
         nc.sync.dma_start(pos1_sb[:], pos1)
         nc.sync.dma_start(pos2_sb[:], pos2)
-        nc.sync.dma_start(out=gate_sb[:], in_=gate.rearrange("g p t -> p g t"))
+        nc.sync.dma_start(out=gate_sb[:], in_=gate[1])
+        with nc.allow_non_contiguous_dma(reason="one gate value a token, tokens on the partitions"):
+            nc.gpsimd.dma_start(out=gate_col[:], in_=gate[0, 0].rearrange("(b p) -> p b", p=P))
 
         def w1_of(e):
-            if e >= EARLY:
-                return early_codes[:, e - EARLY, :], early_plane[:, e - EARLY, :]
+            if e < EARLY:
+                return early_codes[:, e, :], early_plane[:, e, :]
             if e < MIDDLE:
-                return middle_codes[:, e, :], late_plane[:, e, :]
-            return late_codes[:, e - MIDDLE, :], late_plane[:, e, :]
+                return middle_codes[:, e - EARLY, :], late_plane[:, e - EARLY, :]
+            return late_codes[:, e - MIDDLE, :], late_plane[:, e - EARLY, :]
 
         tokens_of = {}
 
         def gather(e0, e1):
             width = C * (e1 - e0)
             entries = offs_sb[:, C * e0 // LIST_ROWS : C * e1 // LIST_ROWS]
-            if (e0, e1) == GATHERS[0]:
-                codes = keep.tile([P, width], U32, name="first_codes", align_bytes=64)
-                plane = keep.tile([P, width], U8, name="first_plane", align_bytes=64)
-            else:
-                codes = code_ring.tile([P, width], U32, name="slot_codes", align_bytes=64)
-                plane = plane_ring.tile([P, width], U8, name="slot_plane", align_bytes=64)
+            codes = ring.tile([P, width], U32, name="slot_codes", align_bytes=64, bufs=3)
+            plane = ring.tile([P, width], U8, name="slot_plane", align_bytes=64)
             nc.vector.tensor_copy(out=codes[:], in_=x_codes[:].bitcast(U32).indirect(entries))
             nc.vector.tensor_copy(out=plane[:], in_=x_plane[:].indirect(entries))
             for e in range(e0, e1):
@@ -119,6 +115,9 @@ def tile_moe_shr_mlp_relu_kernel(
         h_rows_of = {}
 
         def first_layer(e):
+            for e0, e1 in GATHERS:
+                if e0 == e:
+                    gather(e0, e1)
             codes, plane = tokens_of[e]
             w_codes, w_plane = w1_of(e)
             a_sums = psum.tile([C, H], F32, name="a_sums", tag=SUM_BANKS[e])
@@ -180,40 +179,37 @@ def tile_moe_shr_mlp_relu_kernel(
                 second_layer(y_sums[:, (e - e0) * C : (e - e0 + 1) * C], e, *hidden_of[e])
             copy_out(out=y_slots[:, C * e0 : C * e1], in_=y_sums[:, 0 : C * (e1 - e0)])
 
-        for e0, e1 in GATHERS[:3]:
-            gather(e0, e1)
+        first_layer(0)
         for n, experts in enumerate(GROUPS):
-            for e in experts:
-                if e not in h_rows_of:
-                    first_layer(e)
-            if n in (1, 2):
-                gather(*GATHERS[n + 2])
-            if n == 1:
-                first_layer(GROUPS[2][0])
-            if n == len(GROUPS) - 1:
-                slot_results(EARLY, E, "a1", nc.scalar.copy)
-                slot_results(0, 4, "y1", nc.scalar.copy)
-            copy_out = nc.scalar.copy if n < GROUPS_COPIED_BY_SCALAR else nc.vector.tensor_copy
-            turn_and_quantise(experts, TURN_BANKS[n], copy_out)
-        slot_results(4, EARLY, "y2", nc.vector.tensor_copy)
+            for e in range(experts[0] + 1, min(experts[-1] + 2, E)):
+                first_layer(e)
+            copy_out = nc.vector.tensor_copy if n in GROUPS_COPIED_BY_VECTOR else nc.scalar.copy
+            turn_and_quantise(experts, "t%d" % (n % 2), copy_out)
+            if experts[-1] == 5:
+                slot_results(0, 4, "y0", nc.vector.tensor_copy)
+            if experts[-1] == 8:
+                slot_results(4, 8, "y1", nc.scalar.copy)
+        slot_results(8, E, "y2", nc.vector.tensor_copy)
 
         shared_codes = keep.tile([P, PACK, 2 * P], U8, name="shared_codes", align_bytes=64)
         shared_plane = keep.tile([P, PACK, P], U8, name="shared_plane", align_bytes=64)
         w_codes, w_plane = w1_of(E)
-        nc.vector.tensor_copy(
-            out=shared_codes[:].bitcast(U16).rearrange("p d (c m) -> p c d m", m=8),
-            in_=w_codes.bitcast(U16).rearrange("p (c m d) -> p c d m", m=8, d=PACK),
+        nc.gpsimd.tensor_copy(
+            out=shared_codes[:].rearrange("p d (c b) -> p d c b", b=2),
+            in_=w_codes.rearrange("p (c d b) -> p d c b", b=2, d=PACK),
         )
-        nc.vector.tensor_copy(
-            out=shared_plane[:].rearrange("p d (c m) -> p c d m", m=16),
-            in_=w_plane.rearrange("p (c m d) -> p c d m", m=16, d=PACK),
-        )
-        shared_results = []
+        nc.gpsimd.tensor_copy(out=shared_plane[:], in_=w_plane.rearrange("p (c d) -> p d c", d=PACK))
+        def first_choice(t0, t1, tag):
+            picked = keep.tile([N, t1 - t0], F32, name="first", tag=tag, align_bytes=64)
+            nc.vector.tensor_copy(out=picked[:], in_=y_slots[:].indirect(pos1_sb[:, t0 // LIST_ROWS : t1 // LIST_ROWS]))
+            return [picked[:, c : c + C] for c in range(0, t1 - t0, C)]
+
+        shared_hidden = []
         for n, t0 in enumerate(range(0, T, 2 * C)):
             width = min(2 * C, T - t0)
-            grouped = keep.tile([P, width, PACK], BF16, name="grouped_s%d" % t0, align_bytes=64)
+            grouped = keep.tile([P, width, PACK], BF16, name="grouped_s", tag="tail%d" % (n + 1), align_bytes=64)
             for c in range(t0, t0 + width, C):
-                a_sums = psum.tile([P, PACK, C], F32, name="a_sums", tag=SHARED_SUM_BANKS[c // C])
+                a_sums = psum.tile([P, PACK, C], F32, name="a_sums", tag="a%d" % (c // C % 3))
                 for d in range(PACK):
                     nc.tensor.matmul_mx(
                         out=a_sums[:, d, :],
@@ -227,20 +223,44 @@ def tile_moe_shr_mlp_relu_kernel(
                 nc.scalar.activation(
                     out=grouped[:, c - t0 : c - t0 + C, :], in_=a_sums[:].rearrange("q d t -> q t d"), func=RELU
                 )
-            h_codes, h_plane = quantise("_s%d" % t0, grouped[:].rearrange("q t d -> q (t d)"), width)
-            ys_sums = psum.tile([N, 2 * C], F32, name="ys_sums", tag=SHARED_RESULT_BANKS[n])
-            second_layer(ys_sums[:, 0:width], E, h_codes[:], h_plane[:])
-            shared_results.append(ys_sums[:, 0:width])
-
-        first = keep.tile([N, T], F32, name="first")
-        nc.vector.tensor_tensor(out=first[:], in0=y_slots[:].indirect(pos1_sb[:]), in1=gate_sb[:, 0, :], op=MULT)
+            shared_hidden.append(quantise("_s%d" % t0, grouped[:].rearrange("q t d -> q (t d)"), width))
+        first = first_choice(0, 2 * C, "tail0") + first_choice(2 * C, T, "tail1")
         for n, t0 in enumerate(range(0, T, 2 * C)):
-            t1 = min(t0 + 2 * C, T)
-            second = keep.tile([N, t1 - t0], F32, name="second%d" % t0)
-            partial = keep.tile([N, t1 - t0], F32, name="partial%d" % t0)
-            result = keep.tile([N, t1 - t0], F32, name="result%d" % t0)
+            width = min(2 * C, T - t0)
+            t1 = t0 + width
+            blocks = width // C
+            h_codes, h_plane = shared_hidden[n]
+            ys_sums = psum.tile([C, 2, N], F32, name="ys_sums", tag="t%d" % (n % 2))
+            for b in range(blocks):
+                nc.tensor.matmul_mx(
+                    out=ys_sums[:, b, :],
+                    lhsT=h_codes[:, b * C : (b + 1) * C].bitcast(FP8X4),
+                    lhsT_scale=h_plane[:, b * C : (b + 1) * C],
+                    rhs=w2_codes[:, E, :].bitcast(FP4X4),
+                    rhs_scale=w2_plane[:, E, :],
+                    start=True,
+                    stop=True,
+                )
+            ys_rows = keep.tile([C, blocks, N], F32, name="ys_rows%d" % t0)
+            nc.scalar.copy(out=ys_rows[:], in_=ys_sums[:, 0:blocks, :])
+            first_turned = psum.tile([C, 2, N], F32, name="first_turned", tag="y%d" % n)
+            for b in range(blocks):
+                nc.tensor.transpose(first_turned[:, b, :], first[t0 // C + b], identity[:])
+            first_rows = keep.tile([C, blocks, N], F32, name="first_rows%d" % t0)
+            for b in range(blocks):
+                column = t0 // C + b
+                nc.scalar.activation(
+                    out=first_rows[:, b, :], in_=first_turned[:, b, :], func=COPY, scale=gate_col[:, column : column + 1]
+                )
+            partial = psum.tile([N, 2, C], F32, name="partial", tag="y%d" % n)
+            for b in range(blocks):
+                nc.tensor.matmul(partial[:, b, :], lhsT=ys_rows[:, b, :], rhs=identity[:], is_transpose=True, start=True, stop=False)
+                nc.tensor.matmul(partial[:, b, :], lhsT=first_rows[:, b, :], rhs=identity[:], is_transpose=True, start=False, stop=True)
+            second = keep.tile([N, width], F32, name="second", tag="tail%d" % (n + 2), align_bytes=64)
+            result = keep.tile([N, width], F32, name="result%d" % t0)
             entries = pos2_sb[:, t0 // LIST_ROWS : t1 // LIST_ROWS]
-            nc.vector.tensor_tensor(out=second[:], in0=y_slots[:].indirect(entries), in1=gate_sb[:, 1, t0:t1], op=MULT)
-            nc.vector.tensor_tensor(out=partial[:], in0=first[:, t0:t1], in1=shared_results[n], op=ADD)
-            nc.vector.tensor_tensor(out=result[:], in0=partial[:], in1=second[:], op=ADD)
+            nc.vector.tensor_tensor(out=second[:], in0=y_slots[:].indirect(entries), in1=gate_sb[:, t0:t1], op=MULT)
+            nc.vector.tensor_tensor(
+                out=result[:], in0=partial[:, 0:blocks, :].rearrange("n b t -> n (b t)"), in1=second[:], op=ADD
+            )
             nc.sync.dma_start(out=out[:, t0:t1], in_=result[:])

@@ -25,10 +25,13 @@ PACK = 4
 LIST_ROWS = 16
 
 EARLY = 3
-MIDDLE = 7
+MIDDLE = 5
 GATHERS = ((0, 1), (1, 3), (3, 5), (5, 8), (8, 10))
 GROUPS = ((0, 1), (2, 3), (4, 5), (6, 7), (8,), (9,))
 GROUPS_COPIED_BY_VECTOR = (2, 3)
+SHARED_SUM_BANKS = ("y0", "y1", "y0", "y1", "y0")
+RELU_BY_VECTOR = (7,)
+MAX = mybir.AluOpType.max
 SUM_BANKS = ("a0", "a1", "a2", "y2", "y1", "y0", "a0", "a1", "y2", "a2")
 
 
@@ -77,20 +80,20 @@ def tile_moe_shr_mlp_relu_kernel(
             nc.sync.dma_start(out=codes[:].bitcast(I32), in_=words.rearrange("e p b -> p e b").bitcast(I32))
 
         nc.sync.dma_start(offs_sb[:], offs)
-        load_scale_rows(nc.sync, x_plane, x_scales[0])
         nc.sync.dma_start(out=x_codes[:], in_=x_words[0].rearrange("p t r -> p (t r)").bitcast(I32))
+        load_scale_rows(nc.sync, x_plane, x_scales[0])
         load_words(early_codes, w1_words[:EARLY, 0])
         load_scale_rows(nc.sync, early_plane, w1_scales[:EARLY, 0].rearrange("e f i -> f e i"))
         load_words(middle_codes, w1_words[EARLY:MIDDLE, 0])
         load_scale_rows(nc.sync, late_plane, w1_scales[EARLY:, 0].rearrange("e f i -> f e i"))
         load_words(late_codes, w1_words[MIDDLE:, 0])
         load_words(w2_codes, w2_words[:, 0])
-        load_scale_rows(nc.gpsimd, w2_plane, w2_scales[:, 0].rearrange("e f n -> f e n"))
+        load_scale_rows(nc.sync, w2_plane, w2_scales[:, 0].rearrange("e f n -> f e n"))
         nc.sync.dma_start(pos1_sb[:], pos1)
         nc.sync.dma_start(pos2_sb[:], pos2)
         nc.sync.dma_start(out=gate_sb[:], in_=gate[1])
         with nc.allow_non_contiguous_dma(reason="one gate value a token, tokens on the partitions"):
-            nc.gpsimd.dma_start(out=gate_col[:], in_=gate[0, 0].rearrange("(b p) -> p b", p=P))
+            nc.sync.dma_start(out=gate_col[:], in_=gate[0, 0].rearrange("(b p) -> p b", p=P))
 
         def w1_of(e):
             if e < EARLY:
@@ -104,8 +107,8 @@ def tile_moe_shr_mlp_relu_kernel(
         def gather(e0, e1):
             width = C * (e1 - e0)
             entries = offs_sb[:, C * e0 // LIST_ROWS : C * e1 // LIST_ROWS]
-            codes = ring.tile([P, width], U32, name="slot_codes", align_bytes=64, bufs=3)
-            plane = ring.tile([P, width], U8, name="slot_plane", align_bytes=64)
+            codes = ring.tile([P, width], U32, name="slot_codes", align_bytes=64)
+            plane = ring.tile([P, width], U8, name="slot_plane", align_bytes=64, bufs=3)
             nc.vector.tensor_copy(out=codes[:], in_=x_codes[:].bitcast(U32).indirect(entries))
             nc.vector.tensor_copy(out=plane[:], in_=x_plane[:].indirect(entries))
             for e in range(e0, e1):
@@ -131,11 +134,12 @@ def tile_moe_shr_mlp_relu_kernel(
                 stop=True,
             )
             h_rows = keep.tile([C, H], BF16, name="h_rows%d" % e)
-            nc.scalar.activation(
-                out=h_rows[:].rearrange("s (u q d) -> s u q d", u=2, d=2),
-                in_=a_sums[:].rearrange("s (q u d) -> s u q d", u=2, d=2),
-                func=RELU,
-            )
+            pairs_out = h_rows[:].rearrange("s (u q d) -> s u q d", u=2, d=2)
+            pairs_in = a_sums[:].rearrange("s (q u d) -> s u q d", u=2, d=2)
+            if e in RELU_BY_VECTOR:
+                nc.vector.tensor_scalar(out=pairs_out, in0=pairs_in, scalar1=0.0, scalar2=None, op0=MAX)
+            else:
+                nc.scalar.activation(out=pairs_out, in_=pairs_in, func=RELU)
             h_rows_of[e] = h_rows
 
         def quantise(name, grouped, width):
@@ -185,20 +189,21 @@ def tile_moe_shr_mlp_relu_kernel(
                 first_layer(e)
             copy_out = nc.vector.tensor_copy if n in GROUPS_COPIED_BY_VECTOR else nc.scalar.copy
             turn_and_quantise(experts, "t%d" % (n % 2), copy_out)
-            if experts[-1] == 5:
-                slot_results(0, 4, "y0", nc.vector.tensor_copy)
-            if experts[-1] == 8:
-                slot_results(4, 8, "y1", nc.scalar.copy)
+        slot_results(0, 4, "y0", nc.scalar.copy)
+        slot_results(4, 8, "y1", nc.scalar.copy)
         slot_results(8, E, "y2", nc.vector.tensor_copy)
 
         shared_codes = keep.tile([P, PACK, 2 * P], U8, name="shared_codes", align_bytes=64)
         shared_plane = keep.tile([P, PACK, P], U8, name="shared_plane", align_bytes=64)
         w_codes, w_plane = w1_of(E)
-        nc.gpsimd.tensor_copy(
-            out=shared_codes[:].rearrange("p d (c b) -> p d c b", b=2),
-            in_=w_codes.rearrange("p (c d b) -> p d c b", b=2, d=PACK),
+        nc.vector.tensor_copy(
+            out=shared_codes[:].bitcast(U16).rearrange("p d (c m) -> p c d m", m=8),
+            in_=w_codes.bitcast(U16).rearrange("p (c m d) -> p c d m", m=8, d=PACK),
         )
-        nc.gpsimd.tensor_copy(out=shared_plane[:], in_=w_plane.rearrange("p (c d) -> p d c", d=PACK))
+        nc.vector.tensor_copy(
+            out=shared_plane[:].rearrange("p d (c m) -> p c d m", m=16),
+            in_=w_plane.rearrange("p (c m d) -> p c d m", m=16, d=PACK),
+        )
         def first_choice(t0, t1, tag):
             picked = keep.tile([N, t1 - t0], F32, name="first", tag=tag, align_bytes=64)
             nc.vector.tensor_copy(out=picked[:], in_=y_slots[:].indirect(pos1_sb[:, t0 // LIST_ROWS : t1 // LIST_ROWS]))
@@ -209,7 +214,7 @@ def tile_moe_shr_mlp_relu_kernel(
             width = min(2 * C, T - t0)
             grouped = keep.tile([P, width, PACK], BF16, name="grouped_s", tag="tail%d" % (n + 1), align_bytes=64)
             for c in range(t0, t0 + width, C):
-                a_sums = psum.tile([P, PACK, C], F32, name="a_sums", tag="a%d" % (c // C % 3))
+                a_sums = psum.tile([P, PACK, C], F32, name="a_sums", tag=SHARED_SUM_BANKS[c // C])
                 for d in range(PACK):
                     nc.tensor.matmul_mx(
                         out=a_sums[:, d, :],
@@ -230,7 +235,7 @@ def tile_moe_shr_mlp_relu_kernel(
             t1 = t0 + width
             blocks = width // C
             h_codes, h_plane = shared_hidden[n]
-            ys_sums = psum.tile([C, 2, N], F32, name="ys_sums", tag="t%d" % (n % 2))
+            ys_sums = psum.tile([C, 2, N], F32, name="ys_sums", tag=("a0", "a1", "a0")[n])
             for b in range(blocks):
                 nc.tensor.matmul_mx(
                     out=ys_sums[:, b, :],
@@ -243,7 +248,7 @@ def tile_moe_shr_mlp_relu_kernel(
                 )
             ys_rows = keep.tile([C, blocks, N], F32, name="ys_rows%d" % t0)
             nc.scalar.copy(out=ys_rows[:], in_=ys_sums[:, 0:blocks, :])
-            first_turned = psum.tile([C, 2, N], F32, name="first_turned", tag="y%d" % n)
+            first_turned = psum.tile([C, 2, N], F32, name="first_turned", tag=("t0", "t1", "a2")[n])
             for b in range(blocks):
                 nc.tensor.transpose(first_turned[:, b, :], first[t0 // C + b], identity[:])
             first_rows = keep.tile([C, blocks, N], F32, name="first_rows%d" % t0)
@@ -252,7 +257,7 @@ def tile_moe_shr_mlp_relu_kernel(
                 nc.scalar.activation(
                     out=first_rows[:, b, :], in_=first_turned[:, b, :], func=COPY, scale=gate_col[:, column : column + 1]
                 )
-            partial = psum.tile([N, 2, C], F32, name="partial", tag="y%d" % n)
+            partial = psum.tile([N, 2, C], F32, name="partial", tag=("t0", "t1", "a2")[n])
             for b in range(blocks):
                 nc.tensor.matmul(partial[:, b, :], lhsT=ys_rows[:, b, :], rhs=identity[:], is_transpose=True, start=True, stop=False)
                 nc.tensor.matmul(partial[:, b, :], lhsT=first_rows[:, b, :], rhs=identity[:], is_transpose=True, start=False, stop=True)

@@ -24,12 +24,12 @@ P = 128
 PACK = 4
 LIST_ROWS = 16
 
-EARLY = 3
-MIDDLE = 5
+FIRST = 2
+EARLY = 5
 GATHERS = ((0, 1), (1, 3), (3, 5), (5, 8), (8, 10))
 GROUPS = ((0, 1), (2, 3), (4, 5), (6, 7), (8,), (9,))
 GROUPS_COPIED_BY_VECTOR = (2, 3)
-SHARED_SUM_BANKS = ("y0", "y1", "y0", "y1", "y0")
+SHARED_SUM_BANKS = ("y1", "y0", "y2", "y1", "y0")
 RELU_BY_VECTOR = (7,)
 MAX = mybir.AluOpType.max
 SUM_BANKS = ("a0", "a1", "a2", "y2", "y1", "y0", "a0", "a1", "y2", "a2")
@@ -56,10 +56,10 @@ def tile_moe_shr_mlp_relu_kernel(
 
         x_codes = keep.tile([P, T], I32, name="x_codes", align_bytes=64)
         x_plane = keep.tile([P, T], U8, name="x_plane", align_bytes=64)
-        early_codes = keep.tile([P, EARLY, 2 * H], U8, name="early_codes", align_bytes=64)
+        first_codes = keep.tile([P, FIRST, 2 * H], U8, name="first_codes", align_bytes=64)
+        early_codes = keep.tile([P, EARLY - FIRST, 2 * H], U8, name="early_codes", align_bytes=64)
         early_plane = keep.tile([P, EARLY, H], U8, name="early_plane", align_bytes=64)
-        middle_codes = keep.tile([P, MIDDLE - EARLY, 2 * H], U8, name="middle_codes", align_bytes=64)
-        late_codes = keep.tile([P, E + 1 - MIDDLE, 2 * H], U8, name="late_codes", align_bytes=64)
+        late_codes = keep.tile([P, E + 1 - EARLY, 2 * H], U8, name="late_codes", align_bytes=64)
         late_plane = keep.tile([P, E + 1 - EARLY, H], U8, name="late_plane", align_bytes=64)
         w2_codes = keep.tile([P, E + 1, 2 * N], U8, name="w2_codes", align_bytes=64)
         w2_plane = keep.tile([P, E + 1, N], U8, name="w2_plane", align_bytes=64)
@@ -69,26 +69,26 @@ def tile_moe_shr_mlp_relu_kernel(
         identity = keep.tile([P, P], F32, name="identity")
         y_slots = keep.tile([P, SLOTS], F32, name="y_slots")
 
-        nc.gpsimd.memset(x_plane[:].bitcast(I32), 0)
+        nc.vector.memset(x_plane[:].bitcast(I32), 0)
         nc.vector.memset(early_plane[:].bitcast(I32), 0)
+        nc.vector.memset(w2_plane[:].bitcast(I32), 0)
         nc.vector.memset(late_plane[:].bitcast(I32), 0)
         make_identity(nc, ones_diag[:])
-        nc.gpsimd.memset(w2_plane[:].bitcast(I32), 0)
         nc.scalar.activation(out=identity[:], in_=ones_diag[:], func=RELU)
 
         def load_words(codes, words):
             nc.sync.dma_start(out=codes[:].bitcast(I32), in_=words.rearrange("e p b -> p e b").bitcast(I32))
 
         nc.sync.dma_start(offs_sb[:], offs)
-        nc.sync.dma_start(out=x_codes[:], in_=x_words[0].rearrange("p t r -> p (t r)").bitcast(I32))
         load_scale_rows(nc.sync, x_plane, x_scales[0])
-        load_words(early_codes, w1_words[:EARLY, 0])
+        nc.sync.dma_start(out=x_codes[:], in_=x_words[0].rearrange("p t r -> p (t r)").bitcast(I32))
+        load_words(first_codes, w1_words[:FIRST, 0])
         load_scale_rows(nc.sync, early_plane, w1_scales[:EARLY, 0].rearrange("e f i -> f e i"))
-        load_words(middle_codes, w1_words[EARLY:MIDDLE, 0])
-        load_scale_rows(nc.sync, late_plane, w1_scales[EARLY:, 0].rearrange("e f i -> f e i"))
-        load_words(late_codes, w1_words[MIDDLE:, 0])
-        load_words(w2_codes, w2_words[:, 0])
+        load_words(early_codes, w1_words[FIRST:EARLY, 0])
         load_scale_rows(nc.sync, w2_plane, w2_scales[:, 0].rearrange("e f n -> f e n"))
+        load_scale_rows(nc.sync, late_plane, w1_scales[EARLY:, 0].rearrange("e f i -> f e i"))
+        load_words(late_codes, w1_words[EARLY:, 0])
+        load_words(w2_codes, w2_words[:, 0])
         nc.sync.dma_start(pos1_sb[:], pos1)
         nc.sync.dma_start(pos2_sb[:], pos2)
         nc.sync.dma_start(out=gate_sb[:], in_=gate[1])
@@ -96,19 +96,19 @@ def tile_moe_shr_mlp_relu_kernel(
             nc.sync.dma_start(out=gate_col[:], in_=gate[0, 0].rearrange("(b p) -> p b", p=P))
 
         def w1_of(e):
+            if e < FIRST:
+                return first_codes[:, e, :], early_plane[:, e, :]
             if e < EARLY:
-                return early_codes[:, e, :], early_plane[:, e, :]
-            if e < MIDDLE:
-                return middle_codes[:, e - EARLY, :], late_plane[:, e - EARLY, :]
-            return late_codes[:, e - MIDDLE, :], late_plane[:, e - EARLY, :]
+                return early_codes[:, e - FIRST, :], early_plane[:, e, :]
+            return late_codes[:, e - EARLY, :], late_plane[:, e - EARLY, :]
 
         tokens_of = {}
 
         def gather(e0, e1):
             width = C * (e1 - e0)
             entries = offs_sb[:, C * e0 // LIST_ROWS : C * e1 // LIST_ROWS]
-            codes = ring.tile([P, width], U32, name="slot_codes", align_bytes=64)
-            plane = ring.tile([P, width], U8, name="slot_plane", align_bytes=64, bufs=3)
+            codes = ring.tile([P, width], U32, name="slot_codes", align_bytes=64, bufs=3)
+            plane = ring.tile([P, width], U8, name="slot_plane", align_bytes=64)
             nc.vector.tensor_copy(out=codes[:], in_=x_codes[:].bitcast(U32).indirect(entries))
             nc.vector.tensor_copy(out=plane[:], in_=x_plane[:].indirect(entries))
             for e in range(e0, e1):
@@ -153,7 +153,7 @@ def tile_moe_shr_mlp_relu_kernel(
         def turn_and_quantise(experts, bank, copy_out):
             count = len(experts)
             turned = psum.tile([P, 2, 2, C], F32, name="turned", tag=bank)
-            for j, e in enumerate(experts):
+            for j, e in reversed(list(enumerate(experts))):
                 pairs = h_rows_of[e][:].bitcast(F32)
                 for u in range(2):
                     nc.tensor.transpose(turned[:, j, u, :], pairs[:, u * P : (u + 1) * P], identity[:])
@@ -193,8 +193,8 @@ def tile_moe_shr_mlp_relu_kernel(
         slot_results(4, 8, "y1", nc.scalar.copy)
         slot_results(8, E, "y2", nc.vector.tensor_copy)
 
-        shared_codes = keep.tile([P, PACK, 2 * P], U8, name="shared_codes", align_bytes=64)
-        shared_plane = keep.tile([P, PACK, P], U8, name="shared_plane", align_bytes=64)
+        shared_codes = keep.tile([P, PACK, 2 * P], U8, name="shared_codes", tag="grouped8", align_bytes=64)
+        shared_plane = keep.tile([P, PACK, P], U8, name="shared_plane", tag="grouped9", align_bytes=64)
         w_codes, w_plane = w1_of(E)
         nc.vector.tensor_copy(
             out=shared_codes[:].bitcast(U16).rearrange("p d (c m) -> p c d m", m=8),
@@ -229,7 +229,7 @@ def tile_moe_shr_mlp_relu_kernel(
                     out=grouped[:, c - t0 : c - t0 + C, :], in_=a_sums[:].rearrange("q d t -> q t d"), func=RELU
                 )
             shared_hidden.append(quantise("_s%d" % t0, grouped[:].rearrange("q t d -> q (t d)"), width))
-        first = first_choice(0, 2 * C, "tail0") + first_choice(2 * C, T, "tail1")
+        first = first_choice(0, 2 * C, "tail0") + first_choice(2 * C, T, "tail5")
         for n, t0 in enumerate(range(0, T, 2 * C)):
             width = min(2 * C, T - t0)
             t1 = t0 + width
@@ -261,7 +261,7 @@ def tile_moe_shr_mlp_relu_kernel(
             for b in range(blocks):
                 nc.tensor.matmul(partial[:, b, :], lhsT=ys_rows[:, b, :], rhs=identity[:], is_transpose=True, start=True, stop=False)
                 nc.tensor.matmul(partial[:, b, :], lhsT=first_rows[:, b, :], rhs=identity[:], is_transpose=True, start=False, stop=True)
-            second = keep.tile([N, width], F32, name="second", tag="tail%d" % (n + 2), align_bytes=64)
+            second = keep.tile([N, width], F32, name="second", tag=("tail1", "tail3", "tail4")[n], align_bytes=64)
             result = keep.tile([N, width], F32, name="result%d" % t0)
             entries = pos2_sb[:, t0 // LIST_ROWS : t1 // LIST_ROWS]
             nc.vector.tensor_tensor(out=second[:], in0=y_slots[:].indirect(entries), in1=gate_sb[:, t0:t1], op=MULT)

@@ -24,15 +24,15 @@ P = 128
 PACK = 4
 LIST_ROWS = 16
 
-FIRST = 2
-EARLY = 5
+WORD_LOADS = ((0, 2), (2, 5), (5, 8), (8, 11))
+EARLY = 3
 GATHERS = ((0, 1), (1, 3), (3, 5), (5, 8), (8, 10))
 GROUPS = ((0, 1), (2, 3), (4, 5), (6, 7), (8,), (9,))
 GROUPS_COPIED_BY_VECTOR = (2, 3)
-SHARED_SUM_BANKS = ("y1", "y0", "y2", "y1", "y0")
+SHARED_SUM_BANKS = ("y0", "y1", "y2", "y0", "y1")
 RELU_BY_VECTOR = (7,)
 MAX = mybir.AluOpType.max
-SUM_BANKS = ("a0", "a1", "a2", "y2", "y1", "y0", "a0", "a1", "y2", "a2")
+SUM_BANKS = ("a0", "a1", "a2", "a0", "a1", "a2", "a0", "y2", "a1", "a2")
 
 
 def load_scale_rows(queue, plane, rows):
@@ -56,10 +56,10 @@ def tile_moe_shr_mlp_relu_kernel(
 
         x_codes = keep.tile([P, T], I32, name="x_codes", align_bytes=64)
         x_plane = keep.tile([P, T], U8, name="x_plane", align_bytes=64)
-        first_codes = keep.tile([P, FIRST, 2 * H], U8, name="first_codes", align_bytes=64)
-        early_codes = keep.tile([P, EARLY - FIRST, 2 * H], U8, name="early_codes", align_bytes=64)
+        w1_codes = [
+            keep.tile([P, e1 - e0, 2 * H], U8, name="w1_codes%d" % e0, align_bytes=64) for e0, e1 in WORD_LOADS
+        ]
         early_plane = keep.tile([P, EARLY, H], U8, name="early_plane", align_bytes=64)
-        late_codes = keep.tile([P, E + 1 - EARLY, 2 * H], U8, name="late_codes", align_bytes=64)
         late_plane = keep.tile([P, E + 1 - EARLY, H], U8, name="late_plane", align_bytes=64)
         w2_codes = keep.tile([P, E + 1, 2 * N], U8, name="w2_codes", align_bytes=64)
         w2_plane = keep.tile([P, E + 1, N], U8, name="w2_plane", align_bytes=64)
@@ -71,23 +71,27 @@ def tile_moe_shr_mlp_relu_kernel(
 
         nc.vector.memset(x_plane[:].bitcast(I32), 0)
         nc.vector.memset(early_plane[:].bitcast(I32), 0)
-        nc.vector.memset(w2_plane[:].bitcast(I32), 0)
         nc.vector.memset(late_plane[:].bitcast(I32), 0)
+        nc.vector.memset(w2_plane[:].bitcast(I32), 0)
         make_identity(nc, ones_diag[:])
         nc.scalar.activation(out=identity[:], in_=ones_diag[:], func=RELU)
 
         def load_words(codes, words):
             nc.sync.dma_start(out=codes[:].bitcast(I32), in_=words.rearrange("e p b -> p e b").bitcast(I32))
 
+        def load_w1_words(n):
+            load_words(w1_codes[n], w1_words[WORD_LOADS[n][0] : WORD_LOADS[n][1], 0])
+
         nc.sync.dma_start(offs_sb[:], offs)
-        load_scale_rows(nc.sync, x_plane, x_scales[0])
         nc.sync.dma_start(out=x_codes[:], in_=x_words[0].rearrange("p t r -> p (t r)").bitcast(I32))
-        load_words(first_codes, w1_words[:FIRST, 0])
+        load_scale_rows(nc.sync, x_plane, x_scales[0])
+        load_w1_words(0)
         load_scale_rows(nc.sync, early_plane, w1_scales[:EARLY, 0].rearrange("e f i -> f e i"))
-        load_words(early_codes, w1_words[FIRST:EARLY, 0])
-        load_scale_rows(nc.sync, w2_plane, w2_scales[:, 0].rearrange("e f n -> f e n"))
+        load_w1_words(1)
         load_scale_rows(nc.sync, late_plane, w1_scales[EARLY:, 0].rearrange("e f i -> f e i"))
-        load_words(late_codes, w1_words[EARLY:, 0])
+        load_w1_words(2)
+        load_w1_words(3)
+        load_scale_rows(nc.sync, w2_plane, w2_scales[:, 0].rearrange("e f n -> f e n"))
         load_words(w2_codes, w2_words[:, 0])
         nc.sync.dma_start(pos1_sb[:], pos1)
         nc.sync.dma_start(pos2_sb[:], pos2)
@@ -96,19 +100,17 @@ def tile_moe_shr_mlp_relu_kernel(
             nc.sync.dma_start(out=gate_col[:], in_=gate[0, 0].rearrange("(b p) -> p b", p=P))
 
         def w1_of(e):
-            if e < FIRST:
-                return first_codes[:, e, :], early_plane[:, e, :]
-            if e < EARLY:
-                return early_codes[:, e - FIRST, :], early_plane[:, e, :]
-            return late_codes[:, e - EARLY, :], late_plane[:, e - EARLY, :]
+            n = [e0 <= e < e1 for e0, e1 in WORD_LOADS].index(True)
+            plane = early_plane[:, e, :] if e < EARLY else late_plane[:, e - EARLY, :]
+            return w1_codes[n][:, e - WORD_LOADS[n][0], :], plane
 
         tokens_of = {}
 
         def gather(e0, e1):
             width = C * (e1 - e0)
             entries = offs_sb[:, C * e0 // LIST_ROWS : C * e1 // LIST_ROWS]
-            codes = ring.tile([P, width], U32, name="slot_codes", align_bytes=64, bufs=3)
-            plane = ring.tile([P, width], U8, name="slot_plane", align_bytes=64)
+            codes = ring.tile([P, width], U32, name="slot_codes", align_bytes=64)
+            plane = ring.tile([P, width], U8, name="slot_plane", align_bytes=64, bufs=3)
             nc.vector.tensor_copy(out=codes[:], in_=x_codes[:].bitcast(U32).indirect(entries))
             nc.vector.tensor_copy(out=plane[:], in_=x_plane[:].indirect(entries))
             for e in range(e0, e1):
@@ -190,8 +192,8 @@ def tile_moe_shr_mlp_relu_kernel(
             copy_out = nc.vector.tensor_copy if n in GROUPS_COPIED_BY_VECTOR else nc.scalar.copy
             turn_and_quantise(experts, "t%d" % (n % 2), copy_out)
         slot_results(0, 4, "y0", nc.scalar.copy)
-        slot_results(4, 8, "y1", nc.scalar.copy)
-        slot_results(8, E, "y2", nc.vector.tensor_copy)
+        slot_results(4, 8, "y1", nc.vector.tensor_copy)
+        slot_results(8, E, "y2", nc.scalar.copy)
 
         shared_codes = keep.tile([P, PACK, 2 * P], U8, name="shared_codes", tag="grouped8", align_bytes=64)
         shared_plane = keep.tile([P, PACK, P], U8, name="shared_plane", tag="grouped9", align_bytes=64)

@@ -25,14 +25,16 @@ PACK = 4
 LIST_ROWS = 16
 
 WORD_LOADS = ((0, 2), (2, 5), (5, 8), (8, 11))
-EARLY = 3
+EARLY = 5
 GATHERS = ((0, 1), (1, 3), (3, 5), (5, 8), (8, 10))
-GROUPS = ((0, 1), (2, 3), (4, 5), (6, 7), (8,), (9,))
-GROUPS_COPIED_BY_VECTOR = (2, 3)
-SHARED_SUM_BANKS = ("y0", "y1", "y2", "y0", "y1")
-RELU_BY_VECTOR = (7,)
+GROUPS = ((0, 1), (2, 3), (4, 5), (6, 7), (9,), (8,))
+GROUPS_COPIED_BY_VECTOR = (2,)
+SHARED_SUM_BANKS = ("t1", "a2", "a0", "t1", "a2")
+RELU_BY_VECTOR = (7, 9)
 MAX = mybir.AluOpType.max
-SUM_BANKS = ("a0", "a1", "a2", "a0", "a1", "a2", "a0", "y2", "a1", "a2")
+SUM_BANKS = ("a0", "a1", "a2", "a0", "a1", "a2", "a0", "y2", "a1", "y1")
+AHEAD = ((1, 2), (3, 4), (5, 6), (7, 8, 9), (), ())
+TURN_BANKS = ("t0", "t1", "t0", "t1", "a2", "a0")
 
 
 def load_scale_rows(queue, plane, rows):
@@ -71,8 +73,8 @@ def tile_moe_shr_mlp_relu_kernel(
 
         nc.vector.memset(x_plane[:].bitcast(I32), 0)
         nc.vector.memset(early_plane[:].bitcast(I32), 0)
-        nc.vector.memset(late_plane[:].bitcast(I32), 0)
         nc.vector.memset(w2_plane[:].bitcast(I32), 0)
+        nc.vector.memset(late_plane[:].bitcast(I32), 0)
         make_identity(nc, ones_diag[:])
         nc.scalar.activation(out=identity[:], in_=ones_diag[:], func=RELU)
 
@@ -88,10 +90,10 @@ def tile_moe_shr_mlp_relu_kernel(
         load_w1_words(0)
         load_scale_rows(nc.sync, early_plane, w1_scales[:EARLY, 0].rearrange("e f i -> f e i"))
         load_w1_words(1)
-        load_scale_rows(nc.sync, late_plane, w1_scales[EARLY:, 0].rearrange("e f i -> f e i"))
-        load_w1_words(2)
-        load_w1_words(3)
         load_scale_rows(nc.sync, w2_plane, w2_scales[:, 0].rearrange("e f n -> f e n"))
+        load_w1_words(2)
+        load_scale_rows(nc.sync, late_plane, w1_scales[EARLY:, 0].rearrange("e f i -> f e i"))
+        load_w1_words(3)
         load_words(w2_codes, w2_words[:, 0])
         nc.sync.dma_start(pos1_sb[:], pos1)
         nc.sync.dma_start(pos2_sb[:], pos2)
@@ -187,16 +189,16 @@ def tile_moe_shr_mlp_relu_kernel(
 
         first_layer(0)
         for n, experts in enumerate(GROUPS):
-            for e in range(experts[0] + 1, min(experts[-1] + 2, E)):
+            for e in AHEAD[n]:
                 first_layer(e)
             copy_out = nc.vector.tensor_copy if n in GROUPS_COPIED_BY_VECTOR else nc.scalar.copy
-            turn_and_quantise(experts, "t%d" % (n % 2), copy_out)
+            turn_and_quantise(experts, TURN_BANKS[n], copy_out)
         slot_results(0, 4, "y0", nc.scalar.copy)
         slot_results(4, 8, "y1", nc.vector.tensor_copy)
-        slot_results(8, E, "y2", nc.scalar.copy)
+        slot_results(8, E, "y2", nc.vector.tensor_copy)
 
-        shared_codes = keep.tile([P, PACK, 2 * P], U8, name="shared_codes", tag="grouped8", align_bytes=64)
-        shared_plane = keep.tile([P, PACK, P], U8, name="shared_plane", tag="grouped9", align_bytes=64)
+        shared_codes = keep.tile([P, PACK, 2 * P], U8, name="shared_codes", align_bytes=64)
+        shared_plane = keep.tile([P, PACK, P], U8, name="shared_plane", align_bytes=64)
         w_codes, w_plane = w1_of(E)
         nc.vector.tensor_copy(
             out=shared_codes[:].bitcast(U16).rearrange("p d (c m) -> p c d m", m=8),
@@ -237,7 +239,7 @@ def tile_moe_shr_mlp_relu_kernel(
             t1 = t0 + width
             blocks = width // C
             h_codes, h_plane = shared_hidden[n]
-            ys_sums = psum.tile([C, 2, N], F32, name="ys_sums", tag=("a0", "a1", "a0")[n])
+            ys_sums = psum.tile([C, 2, N], F32, name="ys_sums", tag=("a1", "t0", "a1")[n])
             for b in range(blocks):
                 nc.tensor.matmul_mx(
                     out=ys_sums[:, b, :],
@@ -250,7 +252,7 @@ def tile_moe_shr_mlp_relu_kernel(
                 )
             ys_rows = keep.tile([C, blocks, N], F32, name="ys_rows%d" % t0)
             nc.scalar.copy(out=ys_rows[:], in_=ys_sums[:, 0:blocks, :])
-            first_turned = psum.tile([C, 2, N], F32, name="first_turned", tag=("t0", "t1", "a2")[n])
+            first_turned = psum.tile([C, 2, N], F32, name="first_turned", tag="y%d" % n)
             for b in range(blocks):
                 nc.tensor.transpose(first_turned[:, b, :], first[t0 // C + b], identity[:])
             first_rows = keep.tile([C, blocks, N], F32, name="first_rows%d" % t0)
@@ -259,7 +261,7 @@ def tile_moe_shr_mlp_relu_kernel(
                 nc.scalar.activation(
                     out=first_rows[:, b, :], in_=first_turned[:, b, :], func=COPY, scale=gate_col[:, column : column + 1]
                 )
-            partial = psum.tile([N, 2, C], F32, name="partial", tag=("t0", "t1", "a2")[n])
+            partial = psum.tile([N, 2, C], F32, name="partial", tag="y%d" % n)
             for b in range(blocks):
                 nc.tensor.matmul(partial[:, b, :], lhsT=ys_rows[:, b, :], rhs=identity[:], is_transpose=True, start=True, stop=False)
                 nc.tensor.matmul(partial[:, b, :], lhsT=first_rows[:, b, :], rhs=identity[:], is_transpose=True, start=False, stop=True)

@@ -29,12 +29,12 @@ EARLY = 5
 GATHERS = ((0, 1), (1, 3), (3, 5), (5, 8), (8, 10))
 GROUPS = ((0, 1), (2, 3), (4, 5), (6, 7), (9,), (8,))
 GROUPS_COPIED_BY_VECTOR = (2,)
-SHARED_SUM_BANKS = ("t1", "a2", "a0", "t1", "a2")
+SHARED_SUM_BANKS = ("a0", "a1", "a2", "a0", "a1")
 RELU_BY_VECTOR = (7, 9)
 MAX = mybir.AluOpType.max
-SUM_BANKS = ("a0", "a1", "a2", "a0", "a1", "a2", "a0", "y2", "a1", "y1")
-AHEAD = ((1, 2), (3, 4), (5, 6), (7, 8, 9), (), ())
-TURN_BANKS = ("t0", "t1", "t0", "t1", "a2", "a0")
+SUM_BANKS = ("a0", "a1", "a2", "y2", "a0", "t1", "a1", "a2", "y2", "y1")
+AHEAD = ((1, 2, 3), (4, 5, 6), (7, 8, 9), (), (), ())
+TURN_BANKS = ("t0", "t1", "t0", "a0", "a1", "a2")
 
 
 def load_scale_rows(queue, plane, rows):
@@ -239,7 +239,7 @@ def tile_moe_shr_mlp_relu_kernel(
             t1 = t0 + width
             blocks = width // C
             h_codes, h_plane = shared_hidden[n]
-            ys_sums = psum.tile([C, 2, N], F32, name="ys_sums", tag=("a1", "t0", "a1")[n])
+            ys_sums = psum.tile([C, 2, N], F32, name="ys_sums", tag=("t1", "t0", "t1")[n])
             for b in range(blocks):
                 nc.tensor.matmul_mx(
                     out=ys_sums[:, b, :],

@@ -27,14 +27,14 @@ LIST_ROWS = 16
 WORD_LOADS = ((0, 2), (2, 5), (5, 8), (8, 11))
 EARLY = 5
 GATHERS = ((0, 1), (1, 3), (3, 5), (5, 8), (8, 10))
-GROUPS = ((0, 1), (2, 3), (4, 5), (6, 7), (9,), (8,))
+GROUPS = ((0, 1), (2, 3), (4, 5), (6, 7), (8, 9))
 GROUPS_COPIED_BY_VECTOR = (2,)
-SHARED_SUM_BANKS = ("a0", "a1", "a2", "a0", "a1")
-RELU_BY_VECTOR = (7, 9)
+SHARED_SUM_BANKS = ("a0", "a1", "t0", "a0", "a1")
+RELU_BY_VECTOR = (8, 9)
 MAX = mybir.AluOpType.max
 SUM_BANKS = ("a0", "a1", "a2", "y2", "a0", "t1", "a1", "a2", "y2", "y1")
-AHEAD = ((1, 2, 3), (4, 5, 6), (7, 8, 9), (), (), ())
-TURN_BANKS = ("t0", "t1", "t0", "a0", "a1", "a2")
+AHEAD = ((1, 2, 3, 4, 5, 6, 7, 8, 9), (), (), (), (), ())
+TURN_BANKS = ("t0", "t1", "t0", "a0", "a1")
 
 
 def load_scale_rows(queue, plane, rows):
@@ -239,7 +239,7 @@ def tile_moe_shr_mlp_relu_kernel(
             t1 = t0 + width
             blocks = width // C
             h_codes, h_plane = shared_hidden[n]
-            ys_sums = psum.tile([C, 2, N], F32, name="ys_sums", tag=("t1", "t0", "t1")[n])
+            ys_sums = psum.tile([C, 2, N], F32, name="ys_sums", tag=("t1", "a2", "t1")[n])
             for b in range(blocks):
                 nc.tensor.matmul_mx(
                     out=ys_sums[:, b, :],

@@ -16,7 +16,6 @@ U8 = mybir.dt.uint8
 FP8X4 = mybir.dt.float8_e4m3fn_x4
 FP4X4 = mybir.dt.float4_e2m1fn_x4
 RELU = mybir.ActivationFunctionType.Relu
-COPY = mybir.ActivationFunctionType.Copy
 MULT = mybir.AluOpType.mult
 ADD = mybir.AluOpType.add
 
@@ -26,9 +25,9 @@ LIST_ROWS = 16
 
 WORD_LOADS = ((0, 2), (2, 5), (5, 8), (8, 11))
 EARLY = 5
-GATHERS = ((0, 1), (1, 3), (3, 5), (5, 8), (8, 10))
+GATHERS = ((0, 2), (2, 5), (5, 8), (8, 10))
 GROUPS = ((0, 1), (2, 3), (4, 5), (6, 7), (8, 9))
-GROUPS_COPIED_BY_VECTOR = (2,)
+GROUPS_COPIED_BY_VECTOR = ()
 SHARED_SUM_BANKS = ("a0", "a1", "t0", "a0", "a1")
 RELU_BY_VECTOR = (8, 9)
 MAX = mybir.AluOpType.max
@@ -49,7 +48,6 @@ def tile_moe_shr_mlp_relu_kernel(
     with ExitStack() as ctx:
         lists = ctx.enter_context(tc.tile_pool(name="lists", bufs=1))
         keep = ctx.enter_context(tc.tile_pool(name="keep", bufs=1))
-        ring = ctx.enter_context(tc.tile_pool(name="ring", bufs=2))
         psum = ctx.enter_context(tc.psum_pool(name="psum", bufs=1))
 
         offs_sb = lists.tile([P, SLOTS // LIST_ROWS], U16, name="offs_sb")
@@ -65,8 +63,7 @@ def tile_moe_shr_mlp_relu_kernel(
         late_plane = keep.tile([P, E + 1 - EARLY, H], U8, name="late_plane", align_bytes=64)
         w2_codes = keep.tile([P, E + 1, 2 * N], U8, name="w2_codes", align_bytes=64)
         w2_plane = keep.tile([P, E + 1, N], U8, name="w2_plane", align_bytes=64)
-        gate_sb = keep.tile([P, T], F32, name="gate_sb")
-        gate_col = keep.tile([P, T // C], F32, name="gate_col")
+        gate_sb = keep.tile([P, 2, T], F32, name="gate_sb")
         ones_diag = keep.tile([P, P], F32, name="ones_diag")
         identity = keep.tile([P, P], F32, name="identity")
         y_slots = keep.tile([P, SLOTS], F32, name="y_slots")
@@ -84,9 +81,9 @@ def tile_moe_shr_mlp_relu_kernel(
         def load_w1_words(n):
             load_words(w1_codes[n], w1_words[WORD_LOADS[n][0] : WORD_LOADS[n][1], 0])
 
-        nc.sync.dma_start(offs_sb[:], offs)
         nc.sync.dma_start(out=x_codes[:], in_=x_words[0].rearrange("p t r -> p (t r)").bitcast(I32))
         load_scale_rows(nc.sync, x_plane, x_scales[0])
+        nc.sync.dma_start(offs_sb[:], offs)
         load_w1_words(0)
         load_scale_rows(nc.sync, early_plane, w1_scales[:EARLY, 0].rearrange("e f i -> f e i"))
         load_w1_words(1)
@@ -97,9 +94,7 @@ def tile_moe_shr_mlp_relu_kernel(
         load_words(w2_codes, w2_words[:, 0])
         nc.sync.dma_start(pos1_sb[:], pos1)
         nc.sync.dma_start(pos2_sb[:], pos2)
-        nc.sync.dma_start(out=gate_sb[:], in_=gate[1])
-        with nc.allow_non_contiguous_dma(reason="one gate value a token, tokens on the partitions"):
-            nc.sync.dma_start(out=gate_col[:], in_=gate[0, 0].rearrange("(b p) -> p b", p=P))
+        nc.sync.dma_start(out=gate_sb[:], in_=gate.rearrange("r n t -> n r t"))
 
         def w1_of(e):
             n = [e0 <= e < e1 for e0, e1 in WORD_LOADS].index(True)
@@ -111,8 +106,8 @@ def tile_moe_shr_mlp_relu_kernel(
         def gather(e0, e1):
             width = C * (e1 - e0)
             entries = offs_sb[:, C * e0 // LIST_ROWS : C * e1 // LIST_ROWS]
-            codes = ring.tile([P, width], U32, name="slot_codes", align_bytes=64)
-            plane = ring.tile([P, width], U8, name="slot_plane", align_bytes=64, bufs=3)
+            codes = keep.tile([P, width], U32, name="slot_codes%d" % e0, align_bytes=64)
+            plane = keep.tile([P, width], U8, name="slot_plane%d" % e0, align_bytes=64)
             nc.vector.tensor_copy(out=codes[:], in_=x_codes[:].bitcast(U32).indirect(entries))
             nc.vector.tensor_copy(out=plane[:], in_=x_plane[:].indirect(entries))
             for e in range(e0, e1):
@@ -194,7 +189,7 @@ def tile_moe_shr_mlp_relu_kernel(
             copy_out = nc.vector.tensor_copy if n in GROUPS_COPIED_BY_VECTOR else nc.scalar.copy
             turn_and_quantise(experts, TURN_BANKS[n], copy_out)
         slot_results(0, 4, "y0", nc.scalar.copy)
-        slot_results(4, 8, "y1", nc.vector.tensor_copy)
+        slot_results(4, 8, "y1", nc.scalar.copy)
         slot_results(8, E, "y2", nc.vector.tensor_copy)
 
         shared_codes = keep.tile([P, PACK, 2 * P], U8, name="shared_codes", align_bytes=64)
@@ -208,11 +203,6 @@ def tile_moe_shr_mlp_relu_kernel(
             out=shared_plane[:].rearrange("p d (c m) -> p c d m", m=16),
             in_=w_plane.rearrange("p (c m d) -> p c d m", m=16, d=PACK),
         )
-        def first_choice(t0, t1, tag):
-            picked = keep.tile([N, t1 - t0], F32, name="first", tag=tag, align_bytes=64)
-            nc.vector.tensor_copy(out=picked[:], in_=y_slots[:].indirect(pos1_sb[:, t0 // LIST_ROWS : t1 // LIST_ROWS]))
-            return [picked[:, c : c + C] for c in range(0, t1 - t0, C)]
-
         shared_hidden = []
         for n, t0 in enumerate(range(0, T, 2 * C)):
             width = min(2 * C, T - t0)
@@ -233,43 +223,23 @@ def tile_moe_shr_mlp_relu_kernel(
                     out=grouped[:, c - t0 : c - t0 + C, :], in_=a_sums[:].rearrange("q d t -> q t d"), func=RELU
                 )
             shared_hidden.append(quantise("_s%d" % t0, grouped[:].rearrange("q t d -> q (t d)"), width))
-        first = first_choice(0, 2 * C, "tail0") + first_choice(2 * C, T, "tail5")
+
+        def gated_choice(r, t0, t1, tag):
+            picked = keep.tile([N, t1 - t0], F32, name="picked", tag=tag, align_bytes=64)
+            entries = (pos1_sb, pos2_sb)[r][:, t0 // LIST_ROWS : t1 // LIST_ROWS]
+            nc.vector.tensor_tensor(out=picked[:], in0=y_slots[:].indirect(entries), in1=gate_sb[:, r, t0:t1], op=MULT)
+            return picked
+
+        first = gated_choice(0, 0, T, "tail0")
         for n, t0 in enumerate(range(0, T, 2 * C)):
             width = min(2 * C, T - t0)
             t1 = t0 + width
-            blocks = width // C
             h_codes, h_plane = shared_hidden[n]
-            ys_sums = psum.tile([C, 2, N], F32, name="ys_sums", tag=("t1", "a2", "t1")[n])
-            for b in range(blocks):
-                nc.tensor.matmul_mx(
-                    out=ys_sums[:, b, :],
-                    lhsT=h_codes[:, b * C : (b + 1) * C].bitcast(FP8X4),
-                    lhsT_scale=h_plane[:, b * C : (b + 1) * C],
-                    rhs=w2_codes[:, E, :].bitcast(FP4X4),
-                    rhs_scale=w2_plane[:, E, :],
-                    start=True,
-                    stop=True,
-                )
-            ys_rows = keep.tile([C, blocks, N], F32, name="ys_rows%d" % t0)
-            nc.scalar.copy(out=ys_rows[:], in_=ys_sums[:, 0:blocks, :])
-            first_turned = psum.tile([C, 2, N], F32, name="first_turned", tag="y%d" % n)
-            for b in range(blocks):
-                nc.tensor.transpose(first_turned[:, b, :], first[t0 // C + b], identity[:])
-            first_rows = keep.tile([C, blocks, N], F32, name="first_rows%d" % t0)
-            for b in range(blocks):
-                column = t0 // C + b
-                nc.scalar.activation(
-                    out=first_rows[:, b, :], in_=first_turned[:, b, :], func=COPY, scale=gate_col[:, column : column + 1]
-                )
-            partial = psum.tile([N, 2, C], F32, name="partial", tag="y%d" % n)
-            for b in range(blocks):
-                nc.tensor.matmul(partial[:, b, :], lhsT=ys_rows[:, b, :], rhs=identity[:], is_transpose=True, start=True, stop=False)
-                nc.tensor.matmul(partial[:, b, :], lhsT=first_rows[:, b, :], rhs=identity[:], is_transpose=True, start=False, stop=True)
-            second = keep.tile([N, width], F32, name="second", tag=("tail1", "tail3", "tail4")[n], align_bytes=64)
+            ys_sums = psum.tile([N, width], F32, name="ys_sums", tag="y%d" % n)
+            second_layer(ys_sums[:], E, h_codes[:], h_plane[:])
+            second = gated_choice(1, t0, t1, "tail%d" % (n + 4))
+            partial = keep.tile([N, width], F32, name="partial%d" % t0)
             result = keep.tile([N, width], F32, name="result%d" % t0)
-            entries = pos2_sb[:, t0 // LIST_ROWS : t1 // LIST_ROWS]
-            nc.vector.tensor_tensor(out=second[:], in0=y_slots[:].indirect(entries), in1=gate_sb[:, t0:t1], op=MULT)
-            nc.vector.tensor_tensor(
-                out=result[:], in0=partial[:, 0:blocks, :].rearrange("n b t -> n (b t)"), in1=second[:], op=ADD
-            )
+            nc.vector.tensor_tensor(out=partial[:], in0=first[:, t0:t1], in1=second[:], op=ADD)
+            nc.vector.tensor_tensor(out=result[:], in0=ys_sums[:], in1=partial[:], op=ADD)
             nc.sync.dma_start(out=out[:, t0:t1], in_=result[:])

@@ -26,14 +26,17 @@ LIST_ROWS = 16
 WORD_LOADS = ((0, 2), (2, 5), (5, 8), (8, 11))
 EARLY = 5
 GATHERS = ((0, 2), (2, 5), (5, 8), (8, 10))
-GROUPS = ((0, 1), (2, 3), (4, 5), (6, 7), (8, 9))
-GROUPS_COPIED_BY_VECTOR = ()
-SHARED_SUM_BANKS = ("a0", "a1", "t0", "a0", "a1")
+GROUPS = ((0, 1), (2, 3), (4, 5), (6, 7), (9,), (8,))
+GROUPS_COPIED_BY_VECTOR = (0, 4)
+SHARED_SUM_BANKS = ("a0", "a1", "a2", "t0", "t1")
 RELU_BY_VECTOR = (8, 9)
+SHARED_RUNS = ((0, 4 * C), (4 * C, T))
+STORES = ((0, 2 * C), (2 * C, 4 * C), (4 * C, T))
+TAIL_BYTES = 2 * PACK * 2 * C
 MAX = mybir.AluOpType.max
 SUM_BANKS = ("a0", "a1", "a2", "y2", "a0", "t1", "a1", "a2", "y2", "y1")
 AHEAD = ((1, 2, 3, 4, 5, 6, 7, 8, 9), (), (), (), (), ())
-TURN_BANKS = ("t0", "t1", "t0", "a0", "a1")
+TURN_BANKS = ("t0", "t1", "t0", "a0", "a1", "a2")
 
 
 def load_scale_rows(queue, plane, rows):
@@ -48,6 +51,7 @@ def tile_moe_shr_mlp_relu_kernel(
     with ExitStack() as ctx:
         lists = ctx.enter_context(tc.tile_pool(name="lists", bufs=1))
         keep = ctx.enter_context(tc.tile_pool(name="keep", bufs=1))
+        reused = ctx.enter_context(tc.tile_pool(name="reused", bufs=1))
         psum = ctx.enter_context(tc.psum_pool(name="psum", bufs=1))
 
         offs_sb = lists.tile([P, SLOTS // LIST_ROWS], U16, name="offs_sb")
@@ -89,12 +93,13 @@ def tile_moe_shr_mlp_relu_kernel(
         load_w1_words(1)
         load_scale_rows(nc.sync, w2_plane, w2_scales[:, 0].rearrange("e f n -> f e n"))
         load_w1_words(2)
-        load_scale_rows(nc.sync, late_plane, w1_scales[EARLY:, 0].rearrange("e f i -> f e i"))
         load_w1_words(3)
+        load_scale_rows(nc.sync, late_plane, w1_scales[EARLY:, 0].rearrange("e f i -> f e i"))
         load_words(w2_codes, w2_words[:, 0])
         nc.sync.dma_start(pos1_sb[:], pos1)
         nc.sync.dma_start(pos2_sb[:], pos2)
-        nc.sync.dma_start(out=gate_sb[:], in_=gate.rearrange("r n t -> n r t"))
+        for r in range(2):
+            nc.sync.dma_start(out=gate_sb[:, r, :], in_=gate[r])
 
         def w1_of(e):
             n = [e0 <= e < e1 for e0, e1 in WORD_LOADS].index(True)
@@ -156,7 +161,10 @@ def tile_moe_shr_mlp_relu_kernel(
                 pairs = h_rows_of[e][:].bitcast(F32)
                 for u in range(2):
                     nc.tensor.transpose(turned[:, j, u, :], pairs[:, u * P : (u + 1) * P], identity[:])
-            grouped = keep.tile([P, count * C * PACK], BF16, name="grouped%d" % experts[0], align_bytes=64)
+            if experts == GROUPS[-1]:
+                grouped = reused.tile([P, count * C * PACK], BF16, name="grouped_last", align_bytes=64, offset=H)
+            else:
+                grouped = keep.tile([P, count * C * PACK], BF16, name="grouped%d" % experts[0], align_bytes=64)
             copy_out(
                 out=grouped[:].bitcast(F32).rearrange("q (j s u) -> q j s u", j=count, u=2),
                 in_=turned[:, 0:count].rearrange("q j u s -> q j s u"),
@@ -192,8 +200,8 @@ def tile_moe_shr_mlp_relu_kernel(
         slot_results(4, 8, "y1", nc.scalar.copy)
         slot_results(8, E, "y2", nc.vector.tensor_copy)
 
-        shared_codes = keep.tile([P, PACK, 2 * P], U8, name="shared_codes", align_bytes=64)
-        shared_plane = keep.tile([P, PACK, P], U8, name="shared_plane", align_bytes=64)
+        shared_codes = reused.tile([P, PACK, 2 * P], U8, name="shared_codes", align_bytes=64, offset=2 * H)
+        shared_plane = reused.tile([P, PACK, P], U8, name="shared_plane", align_bytes=64, offset=H)
         w_codes, w_plane = w1_of(E)
         nc.vector.tensor_copy(
             out=shared_codes[:].bitcast(U16).rearrange("p d (c m) -> p c d m", m=8),
@@ -203,11 +211,13 @@ def tile_moe_shr_mlp_relu_kernel(
             out=shared_plane[:].rearrange("p d (c m) -> p c d m", m=16),
             in_=w_plane.rearrange("p (c m d) -> p c d m", m=16, d=PACK),
         )
-        shared_hidden = []
-        for n, t0 in enumerate(range(0, T, 2 * C)):
-            width = min(2 * C, T - t0)
-            grouped = keep.tile([P, width, PACK], BF16, name="grouped_s", tag="tail%d" % (n + 1), align_bytes=64)
-            for c in range(t0, t0 + width, C):
+        ys_of = []
+        for t0, t1 in SHARED_RUNS:
+            width = t1 - t0
+            grouped = reused.tile(
+                [P, width, PACK], BF16, name="grouped_s%d" % t0, align_bytes=64, offset=TAIL_BYTES + 2 * PACK * t0
+            )
+            for c in range(t0, t1, C):
                 a_sums = psum.tile([P, PACK, C], F32, name="a_sums", tag=SHARED_SUM_BANKS[c // C])
                 for d in range(PACK):
                     nc.tensor.matmul_mx(
@@ -222,24 +232,21 @@ def tile_moe_shr_mlp_relu_kernel(
                 nc.scalar.activation(
                     out=grouped[:, c - t0 : c - t0 + C, :], in_=a_sums[:].rearrange("q d t -> q t d"), func=RELU
                 )
-            shared_hidden.append(quantise("_s%d" % t0, grouped[:].rearrange("q t d -> q (t d)"), width))
-
-        def gated_choice(r, t0, t1, tag):
-            picked = keep.tile([N, t1 - t0], F32, name="picked", tag=tag, align_bytes=64)
-            entries = (pos1_sb, pos2_sb)[r][:, t0 // LIST_ROWS : t1 // LIST_ROWS]
-            nc.vector.tensor_tensor(out=picked[:], in0=y_slots[:].indirect(entries), in1=gate_sb[:, r, t0:t1], op=MULT)
-            return picked
-
-        first = gated_choice(0, 0, T, "tail0")
-        for n, t0 in enumerate(range(0, T, 2 * C)):
-            width = min(2 * C, T - t0)
-            t1 = t0 + width
-            h_codes, h_plane = shared_hidden[n]
-            ys_sums = psum.tile([N, width], F32, name="ys_sums", tag="y%d" % n)
+            h_codes, h_plane = quantise("_s%d" % t0, grouped[:].rearrange("q t d -> q (t d)"), width)
+            ys_sums = psum.tile([N, width], F32, name="ys_sums", tag="y%d" % len(ys_of))
             second_layer(ys_sums[:], E, h_codes[:], h_plane[:])
-            second = gated_choice(1, t0, t1, "tail%d" % (n + 4))
-            partial = keep.tile([N, width], F32, name="partial%d" % t0)
-            result = keep.tile([N, width], F32, name="result%d" % t0)
-            nc.vector.tensor_tensor(out=partial[:], in0=first[:, t0:t1], in1=second[:], op=ADD)
-            nc.vector.tensor_tensor(out=result[:], in0=ys_sums[:], in1=partial[:], op=ADD)
+            ys_of.append(ys_sums)
+
+        gated = []
+        for r, pos_sb in enumerate((pos1_sb, pos2_sb)):
+            picked = keep.tile([N, T], F32, name="picked%d" % r, align_bytes=64)
+            nc.vector.tensor_tensor(out=picked[:], in0=y_slots[:].indirect(pos_sb[:]), in1=gate_sb[:, r, :], op=MULT)
+            gated.append(picked)
+        routed = reused.tile([N, T], F32, name="routed", align_bytes=64, offset=TAIL_BYTES + 2 * PACK * T - 4 * T)
+        nc.vector.tensor_tensor(out=routed[:], in0=gated[0][:], in1=gated[1][:], op=ADD)
+        for t0, t1 in STORES:
+            run = [s0 <= t0 < s1 for s0, s1 in SHARED_RUNS].index(True)
+            s0 = SHARED_RUNS[run][0]
+            result = keep.tile([N, t1 - t0], F32, name="result%d" % t0)
+            nc.vector.tensor_tensor(out=result[:], in0=ys_of[run][:, t0 - s0 : t1 - s0], in1=routed[:, t0:t1], op=ADD)
             nc.sync.dma_start(out=out[:, t0:t1], in_=result[:])

@@ -28,7 +28,7 @@ EARLY = 5
 GATHERS = ((0, 2), (2, 5), (5, 8), (8, 10))
 GROUPS = ((0, 1), (2, 3), (4, 5), (6, 7), (9,), (8,))
 GROUPS_COPIED_BY_VECTOR = (0, 4)
-SHARED_SUM_BANKS = ("a0", "a1", "a2", "t0", "t1")
+SHARED_SUM_BANKS = ("y0", "y1", "y2", "y0", "y1")
 RELU_BY_VECTOR = (8, 9)
 SHARED_RUNS = ((0, 4 * C), (4 * C, T))
 STORES = ((0, 2 * C), (2 * C, 4 * C), (4 * C, T))
@@ -74,8 +74,8 @@ def tile_moe_shr_mlp_relu_kernel(
 
         nc.vector.memset(x_plane[:].bitcast(I32), 0)
         nc.vector.memset(early_plane[:].bitcast(I32), 0)
-        nc.vector.memset(w2_plane[:].bitcast(I32), 0)
         nc.vector.memset(late_plane[:].bitcast(I32), 0)
+        nc.vector.memset(w2_plane[:].bitcast(I32), 0)
         make_identity(nc, ones_diag[:])
         nc.scalar.activation(out=identity[:], in_=ones_diag[:], func=RELU)
 
@@ -91,10 +91,10 @@ def tile_moe_shr_mlp_relu_kernel(
         load_w1_words(0)
         load_scale_rows(nc.sync, early_plane, w1_scales[:EARLY, 0].rearrange("e f i -> f e i"))
         load_w1_words(1)
-        load_scale_rows(nc.sync, w2_plane, w2_scales[:, 0].rearrange("e f n -> f e n"))
+        load_scale_rows(nc.sync, late_plane, w1_scales[EARLY:, 0].rearrange("e f i -> f e i"))
         load_w1_words(2)
         load_w1_words(3)
-        load_scale_rows(nc.sync, late_plane, w1_scales[EARLY:, 0].rearrange("e f i -> f e i"))
+        load_scale_rows(nc.sync, w2_plane, w2_scales[:, 0].rearrange("e f n -> f e n"))
         load_words(w2_codes, w2_words[:, 0])
         nc.sync.dma_start(pos1_sb[:], pos1)
         nc.sync.dma_start(pos2_sb[:], pos2)
@@ -233,7 +233,7 @@ def tile_moe_shr_mlp_relu_kernel(
                     out=grouped[:, c - t0 : c - t0 + C, :], in_=a_sums[:].rearrange("q d t -> q t d"), func=RELU
                 )
             h_codes, h_plane = quantise("_s%d" % t0, grouped[:].rearrange("q t d -> q (t d)"), width)
-            ys_sums = psum.tile([N, width], F32, name="ys_sums", tag="y%d" % len(ys_of))
+            ys_sums = psum.tile([N, width], F32, name="ys_sums", tag="a%d" % len(ys_of))
             second_layer(ys_sums[:], E, h_codes[:], h_plane[:])
             ys_of.append(ys_sums)
 

@@ -26,8 +26,8 @@ LIST_ROWS = 16
 WORD_LOADS = ((0, 2), (2, 5), (5, 8), (8, 11))
 EARLY = 5
 GATHERS = ((0, 2), (2, 5), (5, 8), (8, 10))
-GROUPS = ((0, 1), (2, 3), (4, 5), (6, 7), (9,), (8,))
-GROUPS_COPIED_BY_VECTOR = (0, 4)
+GROUPS = ((0, 1), (2, 3), (4, 5), (6, 7), (8, 9))
+GROUPS_COPIED_BY_VECTOR = ()
 SHARED_SUM_BANKS = ("y0", "y1", "y2", "y0", "y1")
 RELU_BY_VECTOR = (8, 9)
 SHARED_RUNS = ((0, 4 * C), (4 * C, T))
@@ -162,7 +162,7 @@ def tile_moe_shr_mlp_relu_kernel(
                 for u in range(2):
                     nc.tensor.transpose(turned[:, j, u, :], pairs[:, u * P : (u + 1) * P], identity[:])
             if experts == GROUPS[-1]:
-                grouped = reused.tile([P, count * C * PACK], BF16, name="grouped_last", align_bytes=64, offset=H)
+                grouped = reused.tile([P, count * C * PACK], BF16, name="grouped_last", align_bytes=64, offset=0)
             else:
                 grouped = keep.tile([P, count * C * PACK], BF16, name="grouped%d" % experts[0], align_bytes=64)
             copy_out(
@@ -198,7 +198,7 @@ def tile_moe_shr_mlp_relu_kernel(
             turn_and_quantise(experts, TURN_BANKS[n], copy_out)
         slot_results(0, 4, "y0", nc.scalar.copy)
         slot_results(4, 8, "y1", nc.scalar.copy)
-        slot_results(8, E, "y2", nc.vector.tensor_copy)
+        slot_results(8, E, "y2", nc.scalar.copy)
 
         shared_codes = reused.tile([P, PACK, 2 * P], U8, name="shared_codes", align_bytes=64, offset=2 * H)
         shared_plane = reused.tile([P, PACK, P], U8, name="shared_plane", align_bytes=64, offset=H)

@@ -27,7 +27,7 @@ WORD_LOADS = ((0, 2), (2, 5), (5, 8), (8, 11))
 EARLY = 5
 GATHERS = ((0, 2), (2, 5), (5, 8), (8, 10))
 GROUPS = ((0, 1), (2, 3), (4, 5), (6, 7), (8, 9))
-GROUPS_COPIED_BY_VECTOR = ()
+GROUPS_COPIED_BY_VECTOR = (0,)
 SHARED_SUM_BANKS = ("y0", "y1", "y2", "y0", "y1")
 RELU_BY_VECTOR = (8, 9)
 SHARED_RUNS = ((0, 4 * C), (4 * C, T))

@@ -74,9 +74,10 @@ def tile_moe_shr_mlp_relu_kernel(
 
         nc.vector.memset(x_plane[:].bitcast(I32), 0)
         nc.vector.memset(early_plane[:].bitcast(I32), 0)
+        nc.vector.memset(ones_diag[:], 0.0)
         nc.vector.memset(late_plane[:].bitcast(I32), 0)
         nc.vector.memset(w2_plane[:].bitcast(I32), 0)
-        make_identity(nc, ones_diag[:])
+        make_identity(nc, ones_diag[:], nomemset=True)
         nc.scalar.activation(out=identity[:], in_=ones_diag[:], func=RELU)
 
         def load_words(codes, words):
@@ -242,7 +243,7 @@ def tile_moe_shr_mlp_relu_kernel(
             picked = keep.tile([N, T], F32, name="picked%d" % r, align_bytes=64)
             nc.vector.tensor_tensor(out=picked[:], in0=y_slots[:].indirect(pos_sb[:]), in1=gate_sb[:, r, :], op=MULT)
             gated.append(picked)
-        routed = reused.tile([N, T], F32, name="routed", align_bytes=64, offset=TAIL_BYTES + 2 * PACK * T - 4 * T)
+        routed = reused.tile([N, T], F32, name="routed", align_bytes=64, offset=TAIL_BYTES)
         nc.vector.tensor_tensor(out=routed[:], in0=gated[0][:], in1=gated[1][:], op=ADD)
         for t0, t1 in STORES:
             run = [s0 <= t0 < s1 for s0, s1 in SHARED_RUNS].index(True)

@@ -35,7 +35,7 @@ STORES = ((0, 2 * C), (2 * C, 4 * C), (4 * C, T))
 TAIL_BYTES = 2 * PACK * 2 * C
 MAX = mybir.AluOpType.max
 SUM_BANKS = ("a0", "a1", "a2", "y2", "a0", "t1", "a1", "a2", "y2", "y1")
-AHEAD = ((1, 2, 3, 4, 5, 6, 7, 8, 9), (), (), (), (), ())
+QUANTISED = ((0, 4), (4, 6), (6, 8), (8, 10))
 TURN_BANKS = ("t0", "t1", "t0", "a0", "a1", "a2")
 
 
@@ -155,24 +155,17 @@ def tile_moe_shr_mlp_relu_kernel(
 
         hidden_of = {}
 
-        def turn_and_quantise(experts, bank, copy_out):
+        def turn(experts, bank, grouped, copy_out):
             count = len(experts)
-            turned = psum.tile([P, 2, 2, C], F32, name="turned", tag=bank)
+            turned = psum.tile([P, count, 2, C], F32, name="turned", tag=bank)
             for j, e in reversed(list(enumerate(experts))):
                 pairs = h_rows_of[e][:].bitcast(F32)
                 for u in range(2):
                     nc.tensor.transpose(turned[:, j, u, :], pairs[:, u * P : (u + 1) * P], identity[:])
-            if experts == GROUPS[-1]:
-                grouped = reused.tile([P, count * C * PACK], BF16, name="grouped_last", align_bytes=64, offset=0)
-            else:
-                grouped = keep.tile([P, count * C * PACK], BF16, name="grouped%d" % experts[0], align_bytes=64)
             copy_out(
-                out=grouped[:].bitcast(F32).rearrange("q (j s u) -> q j s u", j=count, u=2),
-                in_=turned[:, 0:count].rearrange("q j u s -> q j s u"),
+                out=grouped.bitcast(F32).rearrange("q (j s u) -> q j s u", j=count, u=2),
+                in_=turned[:].rearrange("q j u s -> q j s u"),
             )
-            h_codes, h_plane = quantise("%d" % experts[0], grouped[:], count * C)
-            for j, e in enumerate(experts):
-                hidden_of[e] = (h_codes[:, j * C : (j + 1) * C], h_plane[:, j * C : (j + 1) * C])
 
         def second_layer(sums, e, h_codes, h_plane):
             nc.tensor.matmul_mx(
@@ -191,12 +184,20 @@ def tile_moe_shr_mlp_relu_kernel(
                 second_layer(y_sums[:, (e - e0) * C : (e - e0 + 1) * C], e, *hidden_of[e])
             copy_out(out=y_slots[:, C * e0 : C * e1], in_=y_sums[:, 0 : C * (e1 - e0)])
 
-        first_layer(0)
-        for n, experts in enumerate(GROUPS):
-            for e in AHEAD[n]:
-                first_layer(e)
-            copy_out = nc.vector.tensor_copy if n in GROUPS_COPIED_BY_VECTOR else nc.scalar.copy
-            turn_and_quantise(experts, TURN_BANKS[n], copy_out)
+        for e in range(E):
+            first_layer(e)
+        for e0, e1 in QUANTISED:
+            if e1 == E:
+                grouped = reused.tile([P, (e1 - e0) * H], BF16, name="grouped_last", align_bytes=64, offset=0)
+            else:
+                grouped = keep.tile([P, (e1 - e0) * H], BF16, name="grouped%d" % e0, align_bytes=64)
+            for n, experts in enumerate(GROUPS):
+                if e0 <= experts[0] < e1:
+                    copy_out = nc.vector.tensor_copy if n in GROUPS_COPIED_BY_VECTOR else nc.scalar.copy
+                    turn(experts, TURN_BANKS[n], grouped[:, (experts[0] - e0) * H : (experts[-1] + 1 - e0) * H], copy_out)
+            h_codes, h_plane = quantise("%d" % e0, grouped[:], (e1 - e0) * C)
+            for e in range(e0, e1):
+                hidden_of[e] = (h_codes[:, (e - e0) * C : (e - e0 + 1) * C], h_plane[:, (e - e0) * C : (e - e0 + 1) * C])
         slot_results(0, 4, "y0", nc.scalar.copy)
         slot_results(4, 8, "y1", nc.scalar.copy)
         slot_results(8, E, "y2", nc.scalar.copy)

@@ -30,8 +30,8 @@ GROUPS = ((0, 1), (2, 3), (4, 5), (6, 7), (8, 9))
 GROUPS_COPIED_BY_VECTOR = (0,)
 SHARED_SUM_BANKS = ("y0", "y1", "y2", "y0", "y1")
 RELU_BY_VECTOR = (8, 9)
-SHARED_RUNS = ((0, 4 * C), (4 * C, T))
-STORES = ((0, 2 * C), (2 * C, 4 * C), (4 * C, T))
+TURNED = 2 * C
+SHARED_RUNS = ((TURNED, 4 * C), (4 * C, T))
 TAIL_BYTES = 2 * PACK * 2 * C
 MAX = mybir.AluOpType.max
 SUM_BANKS = ("a0", "a1", "a2", "y2", "a0", "t1", "a1", "a2", "y2", "y1")
@@ -213,8 +213,8 @@ def tile_moe_shr_mlp_relu_kernel(
             out=shared_plane[:].rearrange("p d (c m) -> p c d m", m=16),
             in_=w_plane.rearrange("p (c m d) -> p c d m", m=16, d=PACK),
         )
-        ys_of = []
-        for t0, t1 in SHARED_RUNS:
+
+        def shared_hidden(t0, t1):
             width = t1 - t0
             grouped = reused.tile(
                 [P, width, PACK], BF16, name="grouped_s%d" % t0, align_bytes=64, offset=TAIL_BYTES + 2 * PACK * t0
@@ -234,21 +234,58 @@ def tile_moe_shr_mlp_relu_kernel(
                 nc.scalar.activation(
                     out=grouped[:, c - t0 : c - t0 + C, :], in_=a_sums[:].rearrange("q d t -> q t d"), func=RELU
                 )
-            h_codes, h_plane = quantise("_s%d" % t0, grouped[:].rearrange("q t d -> q (t d)"), width)
-            ys_sums = psum.tile([N, width], F32, name="ys_sums", tag="a%d" % len(ys_of))
+            return quantise("_s%d" % t0, grouped[:].rearrange("q t d -> q (t d)"), width)
+
+        def gated_choice(r, t0, t1, picked):
+            entries = (pos1_sb, pos2_sb)[r][:, t0 // LIST_ROWS : t1 // LIST_ROWS]
+            nc.vector.tensor_tensor(out=picked[:], in0=y_slots[:].indirect(entries), in1=gate_sb[:, r, t0:t1], op=MULT)
+
+        def add_turned(sums, one, other):
+            nc.tensor.matmul(sums, lhsT=one, rhs=identity[:], is_transpose=True, start=True, stop=False)
+            nc.tensor.matmul(sums, lhsT=other, rhs=identity[:], is_transpose=True, start=False, stop=True)
+
+        early_hidden = shared_hidden(0, TURNED)
+        first = keep.tile([N, T], F32, name="first", align_bytes=64)
+        gated_choice(0, 0, T, first)
+        early_second = keep.tile([N, TURNED], F32, name="early_second", align_bytes=64)
+        gated_choice(1, 0, TURNED, early_second)
+        blocks = [slice(c, c + C) for c in range(0, TURNED, C)]
+        routed_sums = psum.tile([C, TURNED], F32, name="routed_sums", tag="t0")
+        for cols in blocks:
+            add_turned(routed_sums[:, cols], first[:, cols], early_second[:, cols])
+        routed_rows = keep.tile([C, TURNED], F32, name="routed_rows")
+        nc.scalar.copy(out=routed_rows[:], in_=routed_sums[:])
+        ys_sums = psum.tile([C, TURNED], F32, name="ys_sums", tag="t1")
+        for cols in blocks:
+            nc.tensor.matmul_mx(
+                out=ys_sums[:, cols],
+                lhsT=early_hidden[0][:, cols].bitcast(FP8X4),
+                lhsT_scale=early_hidden[1][:, cols],
+                rhs=w2_codes[:, E, :].bitcast(FP4X4),
+                rhs_scale=w2_plane[:, E, :],
+                start=True,
+                stop=True,
+            )
+        ys_rows = keep.tile([C, TURNED], F32, name="ys_rows")
+        nc.scalar.copy(out=ys_rows[:], in_=ys_sums[:])
+        total = psum.tile([N, TURNED], F32, name="total", tag="t0")
+        for cols in blocks:
+            add_turned(total[:, cols], routed_rows[:, cols], ys_rows[:, cols])
+        early_result = keep.tile([N, TURNED], F32, name="early_result")
+        nc.scalar.copy(out=early_result[:], in_=total[:])
+        nc.sync.dma_start(out=out[:, :TURNED], in_=early_result[:])
+
+        ys_of = []
+        for t0, t1 in SHARED_RUNS:
+            h_codes, h_plane = shared_hidden(t0, t1)
+            ys_sums = psum.tile([N, t1 - t0], F32, name="ys_sums", tag="a%d" % len(ys_of))
             second_layer(ys_sums[:], E, h_codes[:], h_plane[:])
             ys_of.append(ys_sums)
-
-        gated = []
-        for r, pos_sb in enumerate((pos1_sb, pos2_sb)):
-            picked = keep.tile([N, T], F32, name="picked%d" % r, align_bytes=64)
-            nc.vector.tensor_tensor(out=picked[:], in0=y_slots[:].indirect(pos_sb[:]), in1=gate_sb[:, r, :], op=MULT)
-            gated.append(picked)
-        routed = reused.tile([N, T], F32, name="routed", align_bytes=64, offset=TAIL_BYTES)
-        nc.vector.tensor_tensor(out=routed[:], in0=gated[0][:], in1=gated[1][:], op=ADD)
-        for t0, t1 in STORES:
-            run = [s0 <= t0 < s1 for s0, s1 in SHARED_RUNS].index(True)
-            s0 = SHARED_RUNS[run][0]
+        second = reused.tile([N, T - TURNED], F32, name="second", align_bytes=64, offset=TAIL_BYTES)
+        gated_choice(1, TURNED, T, second)
+        routed = reused.tile([N, T - TURNED], F32, name="routed", align_bytes=64, offset=TAIL_BYTES + 2 * PACK * TURNED)
+        nc.vector.tensor_tensor(out=routed[:], in0=first[:, TURNED:], in1=second[:], op=ADD)
+        for ys_sums, (t0, t1) in zip(ys_of, SHARED_RUNS):
             result = keep.tile([N, t1 - t0], F32, name="result%d" % t0)
-            nc.vector.tensor_tensor(out=result[:], in0=ys_of[run][:, t0 - s0 : t1 - s0], in1=routed[:, t0:t1], op=ADD)
+            nc.vector.tensor_tensor(out=result[:], in0=ys_sums[:], in1=routed[:, t0 - TURNED : t1 - TURNED], op=ADD)
             nc.sync.dma_start(out=out[:, t0:t1], in_=result[:])

@@ -232,7 +232,9 @@ def tile_moe_shr_mlp_relu_kernel(
                         stop=True,
                     )
                 nc.scalar.activation(
-                    out=grouped[:, c - t0 : c - t0 + C, :], in_=a_sums[:].rearrange("q d t -> q t d"), func=RELU
+                    out=grouped[:, c - t0 : c - t0 + C, :].rearrange("q (g i) d -> q g d i", i=4),
+                    in_=a_sums[:].rearrange("q d (g i) -> q g d i", i=4),
+                    func=RELU,
                 )
             return quantise("_s%d" % t0, grouped[:].rearrange("q t d -> q (t d)"), width)
 

from contextlib import ExitStack

import concourse.mybir as mybir
from concourse.masks import make_identity

K, T, E, C, H, N = 512, 640, 10, 128, 512, 128
SLOTS = E * C
FLOPS = 2 * (SLOTS + T) * (K * H + H * N)

F32 = mybir.dt.float32
BF16 = mybir.dt.bfloat16
I32 = mybir.dt.int32
U32 = mybir.dt.uint32
U16 = mybir.dt.uint16
U8 = mybir.dt.uint8
FP8X4 = mybir.dt.float8_e4m3fn_x4
FP4X4 = mybir.dt.float4_e2m1fn_x4
RELU = mybir.ActivationFunctionType.Relu
MULT = mybir.AluOpType.mult
ADD = mybir.AluOpType.add

P = 128
PACK = 4
LIST_ROWS = 16

WORD_LOADS = ((0, 2), (2, 5), (5, 8), (8, 11))
EARLY = 5
GATHERS = ((0, 2), (2, 5), (5, 8), (8, 10))
GROUPS = ((0, 1), (2, 3), (4, 5), (6, 7), (8, 9))
GROUPS_COPIED_BY_VECTOR = (0,)
SHARED_SUM_BANKS = ("y0", "y1", "y2", "y0", "y1")
RELU_BY_VECTOR = (8, 9)
TURNED = 2 * C
SHARED_RUNS = ((TURNED, 4 * C), (4 * C, T))
TAIL_BYTES = 2 * PACK * 2 * C
MAX = mybir.AluOpType.max
SUM_BANKS = ("a0", "a1", "a2", "y2", "a0", "t1", "a1", "a2", "y2", "y1")
QUANTISED = ((0, 4), (4, 6), (6, 8), (8, 10))
TURN_BANKS = ("t0", "t1", "t0", "a0", "a1", "a2")


def load_scale_rows(queue, plane, rows):
    for r in range(4):
        queue.dma_start(out=plane[r:P:32].bitcast(I32), in_=rows[r:16:4].bitcast(I32))


def tile_moe_shr_mlp_relu_kernel(
    tc, x_words, x_scales, w1_words, w1_scales, w2_words, w2_scales, gate, offs, pos1, pos2, out
):
    nc = tc.nc
    with ExitStack() as ctx:
        lists = ctx.enter_context(tc.tile_pool(name="lists", bufs=1))
        keep = ctx.enter_context(tc.tile_pool(name="keep", bufs=1))
        reused = ctx.enter_context(tc.tile_pool(name="reused", bufs=1))
        psum = ctx.enter_context(tc.psum_pool(name="psum", bufs=1))

        offs_sb = lists.tile([P, SLOTS // LIST_ROWS], U16, name="offs_sb")
        pos1_sb = lists.tile([P, T // LIST_ROWS], U16, name="pos1_sb")
        pos2_sb = lists.tile([P, T // LIST_ROWS], U16, name="pos2_sb")

        x_codes = keep.tile([P, T], I32, name="x_codes", align_bytes=64)
        x_plane = keep.tile([P, T], U8, name="x_plane", align_bytes=64)
        w1_codes = [
            keep.tile([P, e1 - e0, 2 * H], U8, name="w1_codes%d" % e0, align_bytes=64) for e0, e1 in WORD_LOADS
        ]
        early_plane = keep.tile([P, EARLY, H], U8, name="early_plane", align_bytes=64)
        late_plane = keep.tile([P, E + 1 - EARLY, H], U8, name="late_plane", align_bytes=64)
        w2_codes = keep.tile([P, E + 1, 2 * N], U8, name="w2_codes", align_bytes=64)
        w2_plane = keep.tile([P, E + 1, N], U8, name="w2_plane", align_bytes=64)
        gate_sb = keep.tile([P, 2, T], F32, name="gate_sb")
        ones_diag = keep.tile([P, P], F32, name="ones_diag")
        identity = keep.tile([P, P], F32, name="identity")
        y_slots = keep.tile([P, SLOTS], F32, name="y_slots")

        nc.vector.memset(x_plane[:].bitcast(I32), 0)
        nc.vector.memset(early_plane[:].bitcast(I32), 0)
        nc.vector.memset(ones_diag[:], 0.0)
        nc.vector.memset(late_plane[:].bitcast(I32), 0)
        nc.vector.memset(w2_plane[:].bitcast(I32), 0)
        make_identity(nc, ones_diag[:], nomemset=True)
        nc.scalar.activation(out=identity[:], in_=ones_diag[:], func=RELU)

        def load_words(codes, words):
            nc.sync.dma_start(out=codes[:].bitcast(I32), in_=words.rearrange("e p b -> p e b").bitcast(I32))

        def load_w1_words(n):
            load_words(w1_codes[n], w1_words[WORD_LOADS[n][0] : WORD_LOADS[n][1], 0])

        nc.sync.dma_start(out=x_codes[:], in_=x_words[0].rearrange("p t r -> p (t r)").bitcast(I32))
        load_scale_rows(nc.sync, x_plane, x_scales[0])
        nc.sync.dma_start(offs_sb[:], offs)
        load_w1_words(0)
        load_scale_rows(nc.sync, early_plane, w1_scales[:EARLY, 0].rearrange("e f i -> f e i"))
        load_w1_words(1)
        load_scale_rows(nc.sync, late_plane, w1_scales[EARLY:, 0].rearrange("e f i -> f e i"))
        load_w1_words(2)
        load_w1_words(3)
        load_scale_rows(nc.sync, w2_plane, w2_scales[:, 0].rearrange("e f n -> f e n"))
        load_words(w2_codes, w2_words[:, 0])
        nc.sync.dma_start(pos1_sb[:], pos1)
        nc.sync.dma_start(pos2_sb[:], pos2)
        for r in range(2):
            nc.sync.dma_start(out=gate_sb[:, r, :], in_=gate[r])

        def w1_of(e):
            n = [e0 <= e < e1 for e0, e1 in WORD_LOADS].index(True)
            plane = early_plane[:, e, :] if e < EARLY else late_plane[:, e - EARLY, :]
            return w1_codes[n][:, e - WORD_LOADS[n][0], :], plane

        tokens_of = {}

        def gather(e0, e1):
            width = C * (e1 - e0)
            entries = offs_sb[:, C * e0 // LIST_ROWS : C * e1 // LIST_ROWS]
            codes = keep.tile([P, width], U32, name="slot_codes%d" % e0, align_bytes=64)
            plane = keep.tile([P, width], U8, name="slot_plane%d" % e0, align_bytes=64)
            nc.vector.tensor_copy(out=codes[:], in_=x_codes[:].bitcast(U32).indirect(entries))
            nc.vector.tensor_copy(out=plane[:], in_=x_plane[:].indirect(entries))
            for e in range(e0, e1):
                cols = slice(C * (e - e0), C * (e - e0 + 1))
                tokens_of[e] = (codes[:, cols], plane[:, cols])

        h_rows_of = {}

        def first_layer(e):
            for e0, e1 in GATHERS:
                if e0 == e:
                    gather(e0, e1)
            codes, plane = tokens_of[e]
            w_codes, w_plane = w1_of(e)
            a_sums = psum.tile([C, H], F32, name="a_sums", tag=SUM_BANKS[e])
            nc.tensor.matmul_mx(
                out=a_sums[:],
                lhsT=codes.bitcast(FP8X4),
                lhsT_scale=plane,
                rhs=w_codes.bitcast(FP4X4),
                rhs_scale=w_plane,
                start=True,
                stop=True,
            )
            h_rows = keep.tile([C, H], BF16, name="h_rows%d" % e)
            pairs_out = h_rows[:].rearrange("s (u q d) -> s u q d", u=2, d=2)
            pairs_in = a_sums[:].rearrange("s (q u d) -> s u q d", u=2, d=2)
            if e in RELU_BY_VECTOR:
                nc.vector.tensor_scalar(out=pairs_out, in0=pairs_in, scalar1=0.0, scalar2=None, op0=MAX)
            else:
                nc.scalar.activation(out=pairs_out, in_=pairs_in, func=RELU)
            h_rows_of[e] = h_rows

        def quantise(name, grouped, width):
            h_codes = keep.tile([P, width], U32, name="h_codes" + name, align_bytes=64)
            h_plane = keep.tile([P, width], U8, name="h_plane" + name, align_bytes=64)
            nc.vector.quantize_mx(out=h_codes[:].bitcast(FP8X4), scales=h_plane[:], in_=grouped)
            return h_codes, h_plane

        hidden_of = {}

        def turn(experts, bank, grouped, copy_out):
            count = len(experts)
            turned = psum.tile([P, count, 2, C], F32, name="turned", tag=bank)
            for j, e in reversed(list(enumerate(experts))):
                pairs = h_rows_of[e][:].bitcast(F32)
                for u in range(2):
                    nc.tensor.transpose(turned[:, j, u, :], pairs[:, u * P : (u + 1) * P], identity[:])
            copy_out(
                out=grouped.bitcast(F32).rearrange("q (j s u) -> q j s u", j=count, u=2),
                in_=turned[:].rearrange("q j u s -> q j s u"),
            )

        def second_layer(sums, e, h_codes, h_plane):
            nc.tensor.matmul_mx(
                out=sums,
                lhsT=w2_codes[:, e, :].bitcast(FP4X4),
                lhsT_scale=w2_plane[:, e, :],
                rhs=h_codes.bitcast(FP8X4),
                rhs_scale=h_plane,
                start=True,
                stop=True,
            )

        def slot_results(e0, e1, bank, copy_out):
            y_sums = psum.tile([N, 4 * C], F32, name="y_sums", tag=bank)
            for e in range(e0, e1):
                second_layer(y_sums[:, (e - e0) * C : (e - e0 + 1) * C], e, *hidden_of[e])
            copy_out(out=y_slots[:, C * e0 : C * e1], in_=y_sums[:, 0 : C * (e1 - e0)])

        for e in range(E):
            first_layer(e)
        for e0, e1 in QUANTISED:
            if e1 == E:
                grouped = reused.tile([P, (e1 - e0) * H], BF16, name="grouped_last", align_bytes=64, offset=0)
            else:
                grouped = keep.tile([P, (e1 - e0) * H], BF16, name="grouped%d" % e0, align_bytes=64)
            for n, experts in enumerate(GROUPS):
                if e0 <= experts[0] < e1:
                    copy_out = nc.vector.tensor_copy if n in GROUPS_COPIED_BY_VECTOR else nc.scalar.copy
                    turn(experts, TURN_BANKS[n], grouped[:, (experts[0] - e0) * H : (experts[-1] + 1 - e0) * H], copy_out)
            h_codes, h_plane = quantise("%d" % e0, grouped[:], (e1 - e0) * C)
            for e in range(e0, e1):
                hidden_of[e] = (h_codes[:, (e - e0) * C : (e - e0 + 1) * C], h_plane[:, (e - e0) * C : (e - e0 + 1) * C])
        slot_results(0, 4, "y0", nc.scalar.copy)
        slot_results(4, 8, "y1", nc.scalar.copy)
        slot_results(8, E, "y2", nc.scalar.copy)

        shared_codes = reused.tile([P, PACK, 2 * P], U8, name="shared_codes", align_bytes=64, offset=2 * H)
        shared_plane = reused.tile([P, PACK, P], U8, name="shared_plane", align_bytes=64, offset=H)
        w_codes, w_plane = w1_of(E)
        nc.vector.tensor_copy(
            out=shared_codes[:].bitcast(U16).rearrange("p d (c m) -> p c d m", m=8),
            in_=w_codes.bitcast(U16).rearrange("p (c m d) -> p c d m", m=8, d=PACK),
        )
        nc.vector.tensor_copy(
            out=shared_plane[:].rearrange("p d (c m) -> p c d m", m=16),
            in_=w_plane.rearrange("p (c m d) -> p c d m", m=16, d=PACK),
        )

        def shared_hidden(t0, t1):
            width = t1 - t0
            grouped = reused.tile(
                [P, width, PACK], BF16, name="grouped_s%d" % t0, align_bytes=64, offset=TAIL_BYTES + 2 * PACK * t0
            )
            for c in range(t0, t1, C):
                a_sums = psum.tile([P, PACK, C], F32, name="a_sums", tag=SHARED_SUM_BANKS[c // C])
                for d in range(PACK):
                    nc.tensor.matmul_mx(
                        out=a_sums[:, d, :],
                        lhsT=shared_codes[:, d, :].bitcast(FP4X4),
                        lhsT_scale=shared_plane[:, d, :],
                        rhs=x_codes[:, c : c + C].bitcast(FP8X4),
                        rhs_scale=x_plane[:, c : c + C],
                        start=True,
                        stop=True,
                    )
                nc.scalar.activation(
                    out=grouped[:, c - t0 : c - t0 + C, :].rearrange("q (g i) d -> q g d i", i=4),
                    in_=a_sums[:].rearrange("q d (g i) -> q g d i", i=4),
                    func=RELU,
                )
            return quantise("_s%d" % t0, grouped[:].rearrange("q t d -> q (t d)"), width)

        def gated_choice(r, t0, t1, picked):
            entries = (pos1_sb, pos2_sb)[r][:, t0 // LIST_ROWS : t1 // LIST_ROWS]
            nc.vector.tensor_tensor(out=picked[:], in0=y_slots[:].indirect(entries), in1=gate_sb[:, r, t0:t1], op=MULT)

        def add_turned(sums, one, other):
            nc.tensor.matmul(sums, lhsT=one, rhs=identity[:], is_transpose=True, start=True, stop=False)
            nc.tensor.matmul(sums, lhsT=other, rhs=identity[:], is_transpose=True, start=False, stop=True)

        early_hidden = shared_hidden(0, TURNED)
        first = keep.tile([N, T], F32, name="first", align_bytes=64)
        gated_choice(0, 0, T, first)
        early_second = keep.tile([N, TURNED], F32, name="early_second", align_bytes=64)
        gated_choice(1, 0, TURNED, early_second)
        blocks = [slice(c, c + C) for c in range(0, TURNED, C)]
        routed_sums = psum.tile([C, TURNED], F32, name="routed_sums", tag="t0")
        for cols in blocks:
            add_turned(routed_sums[:, cols], first[:, cols], early_second[:, cols])
        routed_rows = keep.tile([C, TURNED], F32, name="routed_rows")
        nc.scalar.copy(out=routed_rows[:], in_=routed_sums[:])
        ys_sums = psum.tile([C, TURNED], F32, name="ys_sums", tag="t1")
        for cols in blocks:
            nc.tensor.matmul_mx(
                out=ys_sums[:, cols],
                lhsT=early_hidden[0][:, cols].bitcast(FP8X4),
                lhsT_scale=early_hidden[1][:, cols],
                rhs=w2_codes[:, E, :].bitcast(FP4X4),
                rhs_scale=w2_plane[:, E, :],
                start=True,
                stop=True,
            )
        ys_rows = keep.tile([C, TURNED], F32, name="ys_rows")
        nc.scalar.copy(out=ys_rows[:], in_=ys_sums[:])
        total = psum.tile([N, TURNED], F32, name="total", tag="t0")
        for cols in blocks:
            add_turned(total[:, cols], routed_rows[:, cols], ys_rows[:, cols])
        early_result = keep.tile([N, TURNED], F32, name="early_result")
        nc.scalar.copy(out=early_result[:], in_=total[:])
        nc.sync.dma_start(out=out[:, :TURNED], in_=early_result[:])

        ys_of = []
        for t0, t1 in SHARED_RUNS:
            h_codes, h_plane = shared_hidden(t0, t1)
            ys_sums = psum.tile([N, t1 - t0], F32, name="ys_sums", tag="a%d" % len(ys_of))
            second_layer(ys_sums[:], E, h_codes[:], h_plane[:])
            ys_of.append(ys_sums)
        second = reused.tile([N, T - TURNED], F32, name="second", align_bytes=64, offset=TAIL_BYTES)
        gated_choice(1, TURNED, T, second)
        routed = reused.tile([N, T - TURNED], F32, name="routed", align_bytes=64, offset=TAIL_BYTES + 2 * PACK * TURNED)
        nc.vector.tensor_tensor(out=routed[:], in0=first[:, TURNED:], in1=second[:], op=ADD)
        for ys_sums, (t0, t1) in zip(ys_of, SHARED_RUNS):
            result = keep.tile([N, t1 - t0], F32, name="result%d" % t0)
            nc.vector.tensor_tensor(out=result[:], in0=ys_sums[:], in1=routed[:, t0 - TURNED : t1 - TURNED], op=ADD)
            nc.sync.dma_start(out=out[:, t0:t1], in_=result[:])
